import numpy as np, ml_dtypes
CORES = [2,6,10,14,18,22,26,30]
N = 8
import mx_ref
BF = ml_dtypes.bfloat16
def gcols(t, e):
    v = np.concatenate([t.reshape(8, 16, -1, 4), np.zeros((8, 16, 1, 4), BF)], axis=2)
    return np.ascontiguousarray(np.stack([v[g][:, e[g]] for g in range(8)])).reshape(128, -1)
def tile(rs):
    return np.stack(rs, axis=2).reshape(128, -1).astype(BF)
def pick(q, e):
    c = np.concatenate([q[0].reshape(128, -1, 4), np.zeros((128, 1, 4), np.uint8)], axis=1); s = np.concatenate([q[1], np.ones((16, 1), np.uint8)], axis=1)
    return (np.ascontiguousarray(c[:, e].reshape(128, -1)), np.ascontiguousarray(s[:, e]))
def join(*qs):
    return (np.concatenate([q[0] for q in qs], axis=1), np.concatenate([q[1] for q in qs], axis=1))
def put(q, e, v):
    c, s = q[0].reshape(128, -1, 4).copy(), q[1].copy(); c[:, e] = v[0].reshape(128, -1, 4); s[:, e] = v[1]
    return (c.reshape(128, -1), s)
def pk(c, s):
    return (np.ascontiguousarray(c), mx_ref.live(s))
def emit(q):
    return q[0], q[1]
def packed(v, rng):
    q = [mx_ref.quantize(np.ascontiguousarray(v[r])) for r in range(N)]
    return np.stack([a for a, b in q]), np.stack([mx_ref.plane(b, rng) for a, b in q])
def values_of_codes():
    e, c = np.zeros((128, 128, 4), np.float32), np.zeros((128, 2, 4), np.uint8)
    e[np.arange(128), np.arange(128), 0] = 1
    c[:127, :, 0] = np.arange(256).reshape(2, 128).T[:127]
    return mx_ref.matmul(mx_ref.quantize(e.reshape(128, 512).astype(BF)), (c.reshape(128, 8), np.full((16, 2), 127, np.uint8))).T.reshape(-1).astype(np.float64)
CODE_VALUE, SCALE_VALUE = values_of_codes(), 2.0 ** (np.arange(256) - 127.0)
def decode(q):
    return (CODE_VALUE[q[0]].reshape(16, 8, -1, 4) * SCALE_VALUE[q[1]][:, None, :, None] + 0.0).reshape(128, -1).astype(np.float32)
def f(rng, *shape):
    return mx_ref.flush((rng.standard_normal(shape, dtype=np.float32) * np.exp2(rng.integers(-2, 3, shape[:-1] + (1,)))).astype(BF))
def wide(rng, *shape, cols=0):
    v = rng.standard_normal(shape, dtype=np.float32) * np.exp2(rng.integers(-12, 13, shape)).astype(np.float32)
    if cols: v *= np.repeat(np.exp2(rng.integers(-cols, cols + 1, shape[:-2] + (1, shape[-1] // 4))) * (rng.random(shape[:-2] + (1, shape[-1] // 4)) > 0.0625), 4, axis=-1).astype(np.float32)
    return mx_ref.flush(v.astype(BF))
C, A, LIFE, T = 384, 128, 128, 10
STEPS = [1, 2]
BEFORE = np.tri(C, k=-1, dtype=bool)
def big(v):
    v = v.astype(np.float32)
    v[np.abs(v) < np.float32(2.0 ** -16)] = 0
    return v.astype(BF)
def numbers_of(rng):
    x = f(rng, N, 128, 4 * C).astype(np.float32) + np.float32(0.5) * np.tile(f(rng, N, 128, 4).astype(np.float32), C)
    return {"x": big(x), "u": np.array(f(rng, N, 128, 512)), "v": np.array(f(rng, N, 128, 512))}
def layers(rng):
    return big(f(rng, N, 128, 2048)).reshape(N, 8, 16, 4, 8, 16, 4)
def weights(rng, w):
    c, p = packed(np.ascontiguousarray(w).reshape(N, 128, 2048), rng)
    return {"wc": c, "ws": p}
def bare(d):
    u = d["u"].astype(np.float32).reshape(N, 8, 16, 128, 4)
    u[:, :, :, np.arange(128) % 16 < 12] = 0
    return d["x"].astype(np.float32).reshape(N, 8, 16, C, 4), u
def planted(rng, d, x, u, w):
    return {"x": x.astype(np.float32).reshape(N, 128, 4 * C).astype(BF), "u": u.reshape(N, 128, 512).astype(BF), "v": d["v"], **weights(rng, w)}
def setup_inputs(rng):
    return {**numbers_of(rng), **weights(rng, layers(rng))}
def setup_inputs_ties(rng):
    d = numbers_of(rng)
    x, u = bare(d)
    o = rng.permutation(N) % 4
    q, half = C // LIFE, LIFE // 2
    sizes = [[LIFE] * q + [0] * (4 - q), [LIFE - 1] * 3 + [C - 3 * (LIFE - 1)], [half] * 3 + [C - 3 * half], [1, 1, 0, C - 2]]
    b = np.arange(4)
    x[:, :, :5] = 0
    for r in range(N):
        shared = [int(g) for g in rng.permutation(8)[:4]] if q == 3 and o[r] == 0 else []
        for g in range(8):
            k = rng.permutation(np.repeat(b, [LIFE, LIFE, half, half] if g in shared else sizes[o[r]]))[:, None]
            top = float(rng.choice([-1.0, 1.0, 2.0]))
            x[r, g, 0] = np.where(b < k, top - 1, np.where(b == k, top, top - rng.integers(0, 2, (C, 4))))
            n = rng.permutation(C)
            x[r, g, 1] = b == (n % 4)[:, None]
            x[r, g, 2, :, 0] = rng.integers(0, 3, C)
            x[r, g, 3, :, 0] = np.where(n < A, 2, 1)
            x[r, g, 4, :, 0] = (n % 4 == 2) & (n < 4 * (T - 1))
            x[r, g, 4, :, 1] = (n % 4 < q) & (n < 4 * (T - 1))
            u[r, g, 3, 16 * g, 0] = 1
            if g in shared: u[r, g, 4, 16 * g + 10:16 * g + 12, 0] = 2048
            elif o[r] == 0: u[r, g, 4, 16 * g + 8:16 * g + 12, 1] = 2048
            for j in range(4):
                u[r, g, 0, 16 * g + 4 + j, j] = 1
                u[r, g, 1, 16 * g + 8 + j, j // 2 if o[r] == 2 else j] = 1024
                u[r, g, 2, 16 * g + 8 + j, 0] = 1
    w = layers(rng)
    w[:, :, :, :, :, :8] = 0
    return planted(rng, d, x, u, w)
def setup_inputs_near(rng):
    d = numbers_of(rng)
    x, u = bare(d)
    o = rng.permutation(N) % 4
    still = [0, 1] + [i for i in range(8, 16)]
    x[:, :, still] = 0
    x[:, :, 0, :, 0] = rng.integers(0, 2, (N, 8, C)) * 2.0 - 1.0
    x[:, :, 1, :, 0] = 2.0 ** -10
    s = rng.integers(0, 16, (N, 8, 4, C))
    x[:, :, 8:12] = ((s[..., None] >> np.arange(4)) & 1) * 2.0 ** (np.arange(4) - 23.0)
    x[:, :, 12] = rng.integers(-1, 2, (N, 8, C, 4)) * 2.0 ** -29
    for r in range(N):
        for g in rng.permutation(8)[:4]: x[r, g, 0, rng.integers(C), 0] = 2.0 ** 29 * float(rng.choice([-1.0, 1.0]))
        k = 1.0 if o[r] == 0 else 2.0 ** -30
        for g in range(8):
            for i in range(9):
                j = (i - 1) % 4
                c = 16 * g + (0 if i == 0 else 3 + i)
                p = 8 if i == 0 else 8 + j if i < 5 else 8 + (j + 1) % 4
                if o[r] < 2:
                    u[r, g, 0, c, 0] = -k if i in (5, 7) else k
                    u[r, g, 1, c, 0] = k
                    u[r, g, p, c] = k
                elif o[r] == 2:
                    if i in (4, 8): u[r, g, 0, c, 0] = 1
                    else: u[r, g, p, c] = k
                else:
                    u[r, g, 12, c, p - 8] = k * (1 + 0.125 * j)
                    if i > 4: u[r, g, 12, c, (p - 7) % 4] = k * 1.125
    w = layers(rng)
    w[:, :, still] = 0
    w[:, :, :, :, :, still] = 0
    return planted(rng, d, x, u, w)
def setup_inputs_late(rng):
    d = numbers_of(rng)
    x, u = bare(d)
    x[:, :, 0] = 0
    e = rng.integers(0, 4, (N, 8))
    for r in range(N):
        for g in range(8): x[r, g, 0, :, e[r, g]] = 2.0 ** -6
    k = 1 + 0.125 * (2 * rng.integers(0, 4, (N, 8, 7, C, 4)) + 1)
    x[:, :, 9:] = k * rng.choice([-1.0, 1.0], k.shape) * 2.0 ** np.array([-14.0, -13.0, -12.0, -11.0, -10.0, -9.0, -8.0])[:, None, None]
    x[:, :, 8] = 0
    x[:, :, 8, :, 0] = 1.96875
    for g in range(8):
        u[:, g, 0, 16 * g] = 1
        for j in range(4):
            u[:, g, 0, 16 * g + 4 + j, j] = 1
            u[:, g, 9 + j, 16 * g + 8 + j] = 1
    w = layers(rng)
    w[:, :, :, :, :, 8:] = 0
    return planted(rng, d, x, u, w)
def setup_inputs_huge(rng):
    d = numbers_of(rng)
    u = bare(d)[1]
    h = rng.permutation(8)
    o = rng.permutation(N) % 3
    most = rng.integers(0, 4, (N, 8, 1, C, 1))
    x = -np.where(np.arange(4) == most, 0.95, 0.75) - 0.05 * rng.random((N, 8, 16, C, 4))
    x[:, h[6:]] *= rng.choice([-1.0, 1.0], (N, 2, 1, C, 1))
    for r in range(N):
        parts = h[6:] if o[r] == 1 else h[:6]
        k = -2.0 ** 30 if o[r] == 2 else 2.0 ** 30
        for g in range(8):
            some = rng.permutation(parts)[:len(parts) // 2]
            for m in parts:
                u[r, m, :, 16 * g] = k * (1 - 0.1 * rng.random((16, 4)))
                for j in range(4):
                    u[r, m, :, 16 * g + 4 + j] = k
                    u[r, m, :, 16 * g + 8 + j] = k
                    if m in some:
                        u[r, m, :, 16 * g + 4 + j, j] = 0.5 * k
                        u[r, m, :, 16 * g + 8 + j, (j + 1) % 4] = 0.5 * k
    a = int(h[0])
    for r in range(N): x[r, a, :, int(rng.integers(C))] = 1.0
    for i in (0, 8, 9, 10, 11):
        u[:, :, :, 16 * a + i] = 0
        u[:, a, :, 16 * a + i] = 2.0 ** 30
    w = np.zeros((N, 128, 4, 128, 4), np.float32)
    i = np.arange(128)
    for b in range(4): w[:, i, b, i, b] = -1
    return planted(rng, d, 2.0 ** 30 * x, u, w.astype(BF))
def setup_inputs_spread(rng):
    d = setup_inputs(rng)
    d["x"] = big(wide(rng, N, 128, 4 * C, cols=6))
    return d
def check_inputs(d):
    b = []
    for k in ("x", "u", "v"):
        a = np.abs(d[k].astype(np.float32))
        if not (np.isfinite(a).all() and ((a == 0) | (a >= 2.0 ** -30) & (a <= 2.0 ** 30)).all()): b.append("a value of " + k)
    none, least, most = [emit(mx_ref.quantize(np.full((128, 16), k, np.float32).astype(BF)))[1][0, 0] for k in (0.0, 2.0 ** -30, 2.0 ** 30)]
    for r in range(N):
        if ((d["wc"][r] == 0x7F) | (d["wc"][r] == 0xFF)).any(): b.append("wc: a code that is no number")
        s = mx_ref.live(d["ws"][r])
        if ((s != none) & ((s < least) | (s > most))).any(): b.append("ws: a scale out of range")
    return b
def reference(x, u, v, wc, ws):
    qu = [mx_ref.quantize(u[r]) for r in range(N)]
    lay = [pk(wc[r], ws[r]) for r in range(N)]
    now = [x[r] for r in range(N)]
    taken = np.zeros((N, 8, C), np.int64)
    g = np.arange(8)
    for step in STEPS:
        score, given = [], []
        for r in range(N):
            s = (mx_ref.matmul(qu[r], mx_ref.quantize(now[r])) + np.float32(0.0)).reshape(8, 16, C)
            o = np.argsort(-s[:, 0], axis=1, kind="stable")[:, :A]
            score.append(s)
            given.append(mx_ref.quantize(gcols(now[r], o)))
        made = []
        for r in range(N):
            came = given[r ^ step]
            objects = decode(came).astype(BF)
            kind = np.argmax(score[r][:, 4:8], axis=1)
            size = np.count_nonzero(kind[:, None] == np.arange(4)[:, None], axis=2)
            stand = np.count_nonzero((kind[:, :, None] == kind[:, None, :]) & BEFORE, axis=2)
            like = (mx_ref.matmul(qu[r], came) + np.float32(0.0)).reshape(8, 16, A)[:, 8:12]
            bites, meals = np.zeros((8, A), np.int64), np.zeros((8, 4, T), np.int64)
            for t in range(T):
                e = np.argmax(np.where((bites < LIFE)[:, None], like, -np.float32(np.inf)), axis=2)
                for k in range(4): bites[g, e[:, k]] += size[:, k]
                meals[:, :, t] = e
            taken[r] = meals[g[:, None], kind, stand % T]
            z = mx_ref.quantize(((now[r].astype(np.float32) + gcols(objects, taken[r]).astype(np.float32)) * np.float32(0.5)).astype(BF))
            made.append(tile([mx_ref.matmul(pick(lay[r], np.arange(128 * b, 128 * b + 128)), z) * np.float32(0.03125) + now[r][:, b::4].astype(np.float32) for b in range(4)]))
        now = made
    y, ol = np.zeros((N, 128, C), np.float32), np.zeros((N, 8, C), np.float32)
    oc, osc = np.zeros((N, 128, 4 * C), np.uint8), np.zeros((N, 16, C), np.uint8)
    for r in range(N):
        q = mx_ref.quantize(now[r])
        y[r] = mx_ref.matmul(mx_ref.quantize(v[r]), q)
        ol[r] = taken[r]
        oc[r], osc[r] = emit(q)
    return {"y": y, "ol": ol, "oc": oc, "osc": osc}

@@ -1,0 +1,478 @@
+from concourse.mybir import dt, AluOpType, ActivationFunctionType
+
+C, A, LIFE, TICKS = 384, 128, 128, 10
+STEPS = [1, 2]
+BIG = 1e29
+EPS = 2.0 ** -100
+F32, BF, I32, U16, X4, U8 = "float32", "bfloat16", "int32", "uint16", "float8_e4m3fn_x4", "uint8"
+QUADS = [([0, 21, 22, 23], 384, 0), ([17, 18, 19, 20], 320, 384), ([13, 14, 15, 16], 256, 704),
+         ([9, 10, 11, 12], 192, 960), ([5, 6, 7, 8], 128, 1152), ([1, 2, 3, 4], 128, 1280)]
+QCOLS, FIRSTV = 1408, 17
+PARTS = {"s64": ("small", 0, 64), "s32": ("small", 64, 32), "f10": ("small", 96, 32), "slot": ("small", 128, 32),
+         "ho": ("hist", 0, TICKS), "ho2": ("hist", TICKS, TICKS), "sgn": ("sm", 0, C)}
+
+
+def _sb(n, d):
+    return ("sbuf", [128, n], d)
+
+
+SCRATCH = {
+    "x0": _sb(4 * C, BF), "x1": _sb(4 * C, BF), "x2": _sb(4 * C, BF),
+    "ut": _sb(512, BF), "vt": _sb(512, BF),
+    "qu": _sb(128, X4), "su": _sb(128, U8), "qv": _sb(128, X4), "sv": _sb(128, U8),
+    "qa": _sb(128, X4), "sa": _sb(128, U8), "qk": _sb(640, X4), "sk": _sb(640, U8),
+    "qw": _sb(512, X4), "sw": _sb(512, U8),
+    "one": _sb(512, BF), "et": _sb(2048, BF), "qe": _sb(512, X4), "se": _sb(512, U8),
+    "grp": _sb(512, BF), "bt": _sb(512, BF), "qb": _sb(128, X4), "sb": _sb(128, U8),
+    "pi": _sb(16, I32), "pf": _sb(16, F32), "col": _sb(16, F32),
+    "g16": _sb(8, F32), "t16": _sb(C, F32), "t4": _sb(128, F32), "num": _sb(400, F32),
+    "uaf": _sb(8, U16), "g40": _sb(40, F32), "uko": _sb(40, U16),
+    "m16": _sb(C, F32), "gate": _sb(C, F32), "start": _sb(C, F32), "keep16": _sb(C, BF),
+    "sel16": _sb(C, F32), "base": _sb(24, F32),
+    "val": _sb(C, F32), "sel": _sb(128, F32), "sel2": _sb(128, F32), "keep4": _sb(32, F32),
+    "c5": _sb(2, F32), "low": _sb(128, F32),
+    "sm": _sb(C, F32), "sx": _sb(C, F32), "dr": _sb(C, BF), "ct": _sb(4 * QCOLS, BF), "cc": _sb(QCOLS, X4),
+    "cs": _sb(QCOLS, U8), "so": _sb((24 - FIRSTV) * 192, BF), "sg": _sb(FIRSTV * 272, BF), "junk": _sb(A * TICKS, BF),
+    "acc": _sb(24, F32), "ra": _sb(96, F32), "ex": _sb(C, F32), "rk": _sb(24, U16),
+    "ord": _sb(C, F32), "osl": _sb(128, F32), "mo": _sb(32, U16),
+    "cq": _sb(C, F32), "cr": _sb(C, F32), "mrt": _sb(C, F32), "d1": _sb(C, BF), "d2": _sb(C, BF),
+    "y1": _sb(C, BF), "y2": _sb(C, BF), "ind": _sb(C, BF), "cnt": _sb(C, F32), "vk": _sb(512, F32),
+    "mu": _sb(2, U16), "mrow": _sb(16, F32), "tab": _sb(1024, F32),
+    "tin": _sb(128, F32), "tout": _sb(128, F32), "small": _sb(160, F32), "fi": _sb(32, I32), "zo": _sb(96, U16),
+    "win": _sb(512, F32), "msk": _sb(128, F32), "rm": _sb(128, F32), "ee": _sb(16, F32), "o5": _sb(2 * TICKS, U16),
+    "cw": _sb(32 * TICKS, F32), "sc": _sb(32, F32), "o1": _sb(8 * TICKS, U16),
+    "bh": _sb(512, F32), "hist": _sb(2 * TICKS, U16), "bm": _sb(160, F32), "erow": _sb(160, F32),
+    "lrow": _sb(C, F32),
+    "xh": _sb(4 * C, BF), "ya": _sb(4 * C, BF), "yb": _sb(4 * C, BF), "yc": _sb(4 * C, BF), "yo": _sb(C, F32),
+    "qx2": _sb(C, X4), "sx2": _sb(C, U8),
+}
+for _r in range(2):
+    SCRATCH.update({"qx%d" % _r: _sb(C, X4), "sx%d" % _r: _sb(C, U8), "mt%d" % _r: _sb(512, BF),
+                    "qm%d" % _r: _sb(A, X4), "sm%d" % _r: _sb(A, U8), "lq%d" % _r: _sb(A, X4), "ls%d" % _r: _sb(A, U8),
+                    "zt%d" % _r: _sb(4 * C, BF), "qz%d" % _r: _sb(C, X4), "sz%d" % _r: _sb(C, U8)})
+for _b in range(8):
+    SCRATCH["ps%d" % _b] = ("psum", [128, 512], F32)
+
+SEMAPHORES = ["V", "S", "P", "G", "lx", "lu", "lv", "lwc", "lws", "tr0", "tr1", "out", "sent", "arr0", "arr1"]
+
+
+def rank_program(g, core, T, topo):
+    rank = T.rank_of(core)
+    if rank is None:
+        return
+    op, fn = AluOpType, ActivationFunctionType
+    queue = {"V": g.vector, "S": g.scalar, "P": g.tensor, "G": g, "Y": g.sync}
+    total = {}
+    known = {q: {} for q in queue}
+    clock = {}
+    touched = {}
+    group = {}
+
+    def v(name, a=0, b=None, s=1, rows=None):
+        if name in PARTS:
+            name, first, n = PARTS[name]
+            a, b = a + first, first + (n if b is None else b)
+        if b is None:
+            b = T[name].shape[1]
+        m = 0
+        if s == 1:
+            m = (1 << b) - (1 << a)
+        else:
+            for i in range(a, b, s):
+                m |= 1 << i
+        r = slice(None) if rows is None else rows
+        return (T[name][r, a:b] if s == 1 else T[name][r, a:b:s], [(name, m)])
+
+    def ind(w, o, cast=None):
+        ap = w[0] if cast is None else w[0].bitcast(cast)
+        return (ap.indirect(o[0]), w[1] + o[1])
+
+    def wait(q, sem, n):
+        if known[q].get(sem, 0) >= n:
+            return
+        queue[q].wait_ge(T.sem[sem], n)
+        known[q][sem] = n
+        for s2, n2 in clock.get((sem, n), {}).items():
+            if known[q].get(s2, 0) < n2:
+                known[q][s2] = n2
+
+    def issue(q, call, writes, reads, sem=None, inc=1, adds=False):
+        sem = sem or q
+        need = {}
+        uses = [(b, m, True) for w in writes for b, m in w[1]]
+        uses += [(b, m, False) for r in reads if isinstance(r, tuple) for b, m in r[1]]
+        for b, m, wr in uses:
+            bank = b.startswith("ps")
+            if bank and adds:
+                continue
+            for s2, n2, m2, w2, q2 in touched.get(b, []):
+                if (bank and (q2 != q or wr or w2)) or (m & m2 and (wr or w2)):
+                    n2 = group.get(s2, n2)
+                    if s2 != sem or s2 not in group:
+                        need[s2] = max(need.get(s2, 0), n2)
+        for s2 in sorted(need, key=lambda z: z == q):
+            wait(q, s2, need[s2])
+        total[sem] = total.get(sem, 0) + inc
+        call().then_inc(T.sem[sem], inc)
+        n = total[sem]
+        key = (sem, group.get(sem, n))
+        old = clock.get(key, {})
+        clock[key] = {z: max(old.get(z, 0), known[q].get(z, 0)) for z in set(old) | set(known[q])}
+        for b, m, wr in uses:
+            lst = touched.setdefault(b, [])
+            if wr:
+                lst[:] = [e for e in lst if e[2] & ~m and not b.startswith("ps")]
+            lst.append((sem, n, m, wr, q))
+
+    def ap(x):
+        return x[0] if isinstance(x, tuple) else x
+
+    def ts(o, i, s1, o0, s2=None, o1=None):
+        if o1 is None:
+            issue("V", lambda: g.vector.tensor_scalar(o[0], i[0], ap(s1), None, o0), [o], [i, s1])
+        else:
+            issue("V", lambda: g.vector.tensor_scalar(o[0], i[0], ap(s1), ap(s2), o0, o1), [o], [i, s1, s2])
+
+    def tt(o, a, b, o0):
+        issue("V", lambda: g.vector.tensor_tensor(o[0], a[0], b[0], o0), [o], [a, b])
+
+    def cp(o, i):
+        issue("V", lambda: g.vector.tensor_copy(o[0], i[0]), [o], [i])
+
+    def scan(o, a, b, init, o0, o1):
+        issue("V", lambda: g.vector.tensor_tensor_scan(o[0], a[0], b[0], ap(init), o0, o1), [o], [a, b, init])
+
+    def fill(o, c):
+        issue("V", lambda: g.vector.memset(o[0], c), [o], [])
+
+    def quant(q, s, i):
+        issue("V", lambda: g.vector.quantize_mx(q[0], s[0], i[0]), [q, s], [i])
+
+    def act(o, i, f, bias=0.0, scale=1.0, acc=None):
+        if f == fn.Copy:
+            issue("S", lambda: g.scalar.activation(o[0], i[0], f), [o], [i])
+        elif acc is None:
+            issue("S", lambda: g.scalar.activation(o[0], i[0], f, bias=ap(bias), scale=ap(scale)), [o], [i, bias, scale])
+        else:
+            issue("S", lambda: g.scalar.activation(o[0], i[0], f, bias=ap(bias), scale=ap(scale), accum_out=acc[0]),
+                  [o, acc], [i, bias, scale])
+
+    def mm(bank, n, wq, ws, xq, xs, start=True, stop=True):
+        o = v("ps%d" % bank, 0, n)
+        issue("P", lambda: g.tensor.matmul_mx(o[0], wq[0], ws[0], xq[0], xs[0], start, stop), [o], [wq, ws, xq, xs],
+              adds=not start)
+
+    def iota(o, pattern, base=0, cm=0, small=True):
+        if small:
+            issue("G", lambda: g.iota(o[0], pattern, base, cm, allow_small_or_imprecise_dtypes=True), [o], [])
+        else:
+            issue("G", lambda: g.iota(o[0], pattern, base, cm), [o], [])
+
+    def dma(q, sem, o, i):
+        issue(q, lambda: queue[q].dma_start(o[0], i[0]), [o], [i], sem=sem, inc=16)
+
+    def ps(b, n=C):
+        return v("ps%d" % b, 0, n)
+
+    def col(name, j):
+        return v(name, j, j + 1)
+
+    def bytes_of(x):
+        return (x[0].bitcast(dt.uint8), x[1])
+
+    def words_of(x):
+        return (x[0].bitcast(dt.uint32), x[1])
+
+    group["tr0"] = group["tr1"] = 8 * 16
+    group["out"] = 9 * 16
+
+    dma("S", "lu", v("ut"), (T.u[:, :], []))
+    dma("Y", "lx", v("x0"), (T.x[:, :], []))
+    dma("Y", "lwc", bytes_of(v("qw")), (T.wc[:, :], []))
+    dma("Y", "lws", v("sw"), (T.ws[:, :], []))
+    dma("Y", "lv", v("vt"), (T.v[:, :], []))
+
+    iota(v("g16"), [[16, 8]])
+    iota(col("pi", 0), [[0, 1]], 0, 1, small=False)
+    iota(v("t16"), [[0, 24], [1, 16]])
+    iota(v("g40"), [[1, 5], [16, 8]], 4)
+    iota(v("grp"), [[16, 8], [0, 64]])
+    iota(v("t4"), [[0, 32], [1, 4]])
+    iota(v("num"), [[1, 400]])
+    fill(v("one"), 1.0)
+    cp(v("uaf"), v("g16"))
+    ts(col("pi", 1), col("pi", 0), 15, op.bitwise_and)
+    ts(col("pi", 2), col("pi", 0), 3, op.bitwise_and)
+    ts(col("pi", 3), col("pi", 0), 2, op.logical_shift_right, 3, op.bitwise_and)
+    ts(col("pi", 4), col("pi", 0), 1, op.bitwise_and)
+    ts(col("pi", 5), col("pi", 0), 2, op.bitwise_and)
+    ts(col("pi", 6), col("pi", 0), 112, op.bitwise_and)
+    cp(v("pf", 0, 7), v("pi", 0, 7))
+    cq, ck, cr, b1, b2 = col("pf", 1), col("pf", 2), col("pf", 3), col("pf", 4), col("pf", 5)
+    for ks, n, c0 in QUADS[:3]:
+        fill(v("ct", 4 * (c0 + n - 48), 4 * (c0 + n)), 0.0)
+    ts(v("m16"), v("t16"), cq, op.is_equal)
+    for ks, n, c0 in QUADS[3:]:
+        fill(v("ct", 4 * (c0 + 16 * ks[0]), 4 * (c0 + n)), 0.0)
+    for b in range(4):
+        issue("G", lambda b=b: g.affine_select(T.et[:, 512 * b:512 * b + 512], T.one[:, :], [[-1, 512]], op.is_equal, 0.0, b, 4),
+              [v("et", 512 * b, 512 * b + 512)], [v("one")])
+    for name, n in (("win", 512), ("low", 128)):
+        issue("G", lambda name=name, n=n: g.affine_select(T[name][:, :], T.one[:, 0:n], [[0, n]], op.is_equal, -BIG, 1, 0),
+              [v(name)], [v("one")])
+    iota(v("tab"), [[0, 1024]])
+    iota(v("vk", C, 512), [[0, 128]])
+    iota(v("cw", 0, 32), [[0, 32]])
+    ts(v("uko", 0, 8), v("g40", 0, 8), ck, op.add)
+    ts(v("uko", 8, 16), v("g40", 8, 16), b2, op.add, b1, op.subtract)
+    ts(v("uko", 16, 24), v("g40", 16, 24), b1, op.add, b2, op.subtract)
+    ts(v("uko", 24, 32), v("g40", 24, 32), ck, op.subtract)
+    ts(v("uko", 32, 40), v("g40", 32, 40), ck, op.add)
+    act(col("acc", 0), ck, fn.Identity, scale=0.0)
+    act(v("start"), v("t16"), fn.Identity, bias=-BIG, scale=2 * BIG)
+    act(v("keep16"), v("t16"), fn.Sign)
+    act(v("gate"), v("m16"), fn.Identity, bias=-BIG, scale=2 * BIG)
+
+    def keeper(out, sign, tmp, run):
+        act(v(tmp), v(sign), fn.Abs, bias=-0.5, scale=-8192.0)
+        act(v(out), v(tmp), fn.Relu, bias=8192.5, scale=-1.0)
+        act(v(out, run - 1, None, run), v(sign, run - 1, None, run), fn.Identity, bias=2.0 ** -13, scale=2.0 ** -13 - 2.0 ** -26)
+
+    def later_constants():
+        act(col("col", 2), b1, fn.Identity, bias=EPS, scale=-2.0 * EPS)
+        act(col("col", 3), b2, fn.Identity, bias=EPS, scale=-EPS)
+        act(col("col", 4), ck, fn.Identity, bias=-1.0, scale=1.0 / 16)
+        act(col("col", 5), ck, fn.Identity, bias=1.0, scale=-1.0 / 16)
+        act(col("col", 6), cq, fn.Identity, bias=-63.5 / 128, scale=4.0)
+        act(col("col", 7), cr, fn.Identity, bias=112.0, scale=-16.0)
+        act(v("keep4"), v("t4", 0, 32), fn.Sign)
+        act(col("c5", 0), ck, fn.Identity, bias=col("col", 7), scale=256.0)
+        act(v("cw", 0, 32, 4), v("g16"), fn.Identity, bias=col("col", 6), scale=4.0)
+        act(col("c5", 1), col("c5", 0), fn.Identity, bias=-64.0)
+
+    quant(v("qu"), v("su"), v("ut"))
+    cp(words_of(v("qa")), ind(v("qu"), v("uaf"), dt.uint32))
+    act(v("sa"), ind(v("su"), v("uaf")), fn.Copy)
+    ts(v("bt"), v("grp"), col("pf", 6), op.is_equal)
+    cp(words_of(v("qk", 0, 320)), ind(v("qu"), v("uko", 0, 20), dt.uint32))
+    quant(v("qb"), v("sb"), v("bt"))
+    act(v("sgn"), v("t16"), fn.Sign, bias=cq, scale=-1.0)
+    act(v("sk", 0, 320), ind(v("su"), v("uko", 0, 20)), fn.Copy)
+    keeper("sel16", "sgn", "ex", 16)
+    act(v("sk", 320, 640), ind(v("su"), v("uko", 20, 40)), fn.Copy)
+
+    far = [T.cores[rank ^ s] for s in STEPS]
+    mask = topo.mask(core, far[0])
+    for p in far[1:]:
+        mask &= topo.mask(core, p)
+    engines = bin(mask).count("1")
+
+    def uk(j):
+        return v("qk", 128 * j, 128 * j + 128), v("sk", 128 * j, 128 * j + 128)
+
+    place = {k: (c0, s) for ks, n, c0 in QUADS for s, k in enumerate(ks)}
+
+    def cmp_view(k, a, b):
+        c0, s = place[k]
+        return v("ct", 4 * (c0 + a) + s, 4 * (c0 + b), 4)
+
+    xs, ys = ["x0", "x1", "x2"], ["ya", "yb", "yc"]
+    quant(v("qx0"), v("sx0"), v("x0"))
+    for r in range(2):
+        X, Y = xs[r], ys[r]
+        qx, sx = v("qx%d" % r), v("sx%d" % r)
+        mm(1, C, v("qa"), v("sa"), qx, sx)
+        mm(0, C, v("qa"), v("sa"), qx, sx)
+        if r == 0:
+            cp(words_of(v("qk", 320, 640)), ind(v("qu"), v("uko", 20, 40), dt.uint32))
+        parts = ((208, 272), (0, 208), (272, C))
+        for a, b in parts:
+            tt(v("sm", a, b), v("ps1", a, b), v("gate", a, b), op.min)
+        for a, b in parts:
+            scan(v("sx", a, b), v("start", a, b), v("sm", a, b), -BIG, op.min, op.max)
+        for j in range(4):
+            mm(2 + j, C, uk(j)[0], uk(j)[1], qx, sx)
+
+        def compare(k):
+            ts(cmp_view(k, 0, 16 * k), v("ps1", 0, 16 * k), col("sx", 16 * k + 15), op.is_lt)
+
+        def count(k):
+            e = 192 * (k - FIRSTV + 1)
+            scan(v("so", e - 8 * k, e), cmp_view(k, 0, 8 * k), cmp_view(k, 8 * k, 16 * k), -192.0, op.add, op.add)
+
+        def quad(i):
+            ks, n, c0 = QUADS[i]
+            quant(v("cc", c0, c0 + n), v("cs", c0, c0 + n), v("ct", 4 * c0, 4 * (c0 + n)))
+            mm(6, n, v("qb"), v("sb"), v("cc", c0, c0 + n), v("cs", c0, c0 + n), i == 0, i == len(QUADS) - 1)
+
+        def sign(k):
+            act(v("sg", 272 * k, 272 * k + 16 * k), v("ps0", 0, 16 * k), fn.Sign, bias=col("sx", 16 * k + 15), scale=-1.0)
+
+        sign(FIRSTV - 1)
+        for k in range(FIRSTV - 1, 0, -1):
+            if k > 1:
+                sign(k - 1)
+            act(cmp_view(k, 0, 16 * k), v("sg", 272 * k, 272 * k + 16 * k), fn.Relu, acc=col("acc", k))
+        if r == 0:
+            act(v("val"), v("num", 0, C), fn.Identity, bias=ck, scale=4.0)
+            act(v("sel2"), v("t4"), fn.Sign, bias=cr, scale=-1.0)
+            keeper("sel", "sel2", "osl", 4)
+        act(v("cq"), ps(3), fn.Copy)
+        act(v("cr"), ps(4), fn.Copy)
+
+        tt(cmp_view(0, 0, C), ps(1), v("sx"), op.is_le)
+        compare(23)
+        if r == 0:
+            ts(v("base", 0, FIRSTV), v("num", 0, 16 * FIRSTV, 16), cq, op.subtract, 14.625, op.add)
+            ts(v("base", FIRSTV, 24), v("num", 16 * FIRSTV, C, 16), cq, op.subtract, 14.625 - 192, op.add)
+        scan(v("dr"), v("keep16"), cmp_view(0, 0, C), 0.0, op.mult, op.add)
+        compare(22)
+        count(23)
+        compare(21)
+        count(22)
+        tt(v("ra", 0, 24), v("base"), v("dr", 15, C, 16), op.subtract)
+        count(21)
+        quad(0)
+        compare(20)
+        quad(2)
+        for k in (19, 18, 17):
+            compare(k)
+            count(k + 1)
+        count(17)
+        quad(1)
+        quad(3)
+        cp(v("acc", FIRSTV, 24), v("so", 191, None, 192))
+        quad(4)
+        quad(5)
+        tt(v("ra", 24, 48), v("ra", 0, 24), v("acc"), op.subtract)
+        if r == 0:
+            quant(v("qe", 0, 256), v("se", 0, 256), v("et", 0, 1024))
+        ts(v("ra", 48, 72), v("ra", 24, 48), 2.0 ** -13, op.mult)
+        scan(v("ex"), ps(6), v("sel16"), 0.0, op.add, op.mult)
+        tt(v("ra", 72, 96), v("ex", 15, C, 16), v("ra", 48, 72), op.add)
+        ts(v("rk"), v("ra", 72, 96), 8192.0, op.mult)
+        o = ind(v("ord"), v("rk"))
+        issue("V", lambda o=o: g.vector.tensor_copy(o[0], T.val[:, :]), [v("ord")], [v("rk"), v("val")])
+        scan(v("osl"), v("ord", 0, 128), v("sel"), 0.0, op.add, op.mult)
+        ts(v("mo"), v("osl", 3, 128, 4), 8192.0, op.mult, -0.375, op.add)
+        mt = "mt%d" % r
+        act(v(mt, 256, 512), ind(v(X), v("mo", 16, 32)), fn.Copy)
+        cp(v(mt, 0, 256), ind(v(X), v("mo", 0, 16)))
+        if r == 0:
+            later_constants()
+        qm, sm, lq, ls = v("qm%d" % r), v("sm%d" % r), v("lq%d" % r), v("ls%d" % r)
+        quant(qm, sm, v(mt))
+        wait("G", "V", total["V"])
+        rid, pid = topo.addr(far[r])[:2]
+        arr = "arr%d" % r
+        g.remote_dma(lq[0].bitcast(dt.uint8), qm[0].bitcast(dt.uint8), T.sem[arr], T.sem.sent, pid, rid, mask)
+        g.remote_dma(ls[0], sm[0], T.sem[arr], T.sem.sent, pid, rid, mask)
+
+        tt(v("d1"), ps(2), v("cq"), op.subtract)
+        tt(v("mrt"), ps(5), v("cr"), op.max)
+        act(v("y1"), v("d1"), fn.Sign, bias=col("col", 2))
+        tt(v("d2"), ps(2), v("mrt"), op.subtract)
+        ts(v("y2"), v("d2"), col("col", 3), op.add, 0.0, op.is_gt)
+        tt(v("ind"), v("y1"), v("y2"), op.is_equal)
+        scan(v("cnt"), v("ind"), v("one", 0, C), col("col", 4), op.add, op.mult)
+        ts(col("mu", 0), col("cnt", C - 1), col("col", 5), op.add)
+        ts(v("mrow"), ind(v("num"), col("mu", 0)), 1.0 / LIFE, op.mult)
+        tt(v("vk", 0, C), v("cnt"), v("ind"), op.mult)
+        for k in range(4):
+            act(v("tab", 256 * k + 112, 256 * k + 128), v("m16", 0, 16), fn.Identity, scale=col("mrow", k))
+        for h in range(2):
+            for k in range(4):
+                dma("Y", "tr%d" % r, v("tin", 32 * k + 16 * h, 32 * k + 16 * h + 16),
+                    v("vk", rows=slice(16 * h + k, 128, 32)))
+
+        wait("P", arr, 2 * engines)
+        mm(1, A, uk(4)[0], uk(4)[1], lq, ls)
+        mm(0, A, uk(4)[0], uk(4)[1], lq, ls)
+        act(v("win", 0, 512, 4), ps(0, A), fn.Copy)
+
+        def objects():
+            if r == 0:
+                quant(v("qe", 256, 512), v("se", 256, 512), v("et", 1024, 2048))
+            for b in range(4):
+                mm(2 + b, A, v("qe", 128 * b, 128 * b + 128), v("se", 128 * b, 128 * b + 128), lq, ls)
+
+        spare_s = {t: [] for t in range(TICKS)}
+        for b in range(4):
+            spare_s[b + 1].append(lambda b=b: act(v("bh", b, 512, 4), ps(2 + b, A), fn.Identity, scale=0.5))
+            if r == 0:
+                spare_s[b].append(lambda b=b: act(v("ya", C * b, C * b + C), v(X, b, 4 * C, 4), fn.Identity, scale=32.0))
+            spare_s[b + 4].append(lambda b=b: act(v("xh", C * b, C * b + C), v(Y, C * b, C * b + C), fn.Identity, scale=1.0 / 64))
+        spare_s[8].append(lambda: act(v("bm", 0, 128), ind(v("bh"), v("ho", 0, 8)), fn.Copy))
+        spare_v = {
+            0: [objects],
+            1: [lambda: quant(v("qv"), v("sv"), v("vt"))] if r == 0 else [],
+            2: [lambda: issue("V", lambda: g.vector.transpose(T.tout[:, :], T.tin[:, :]), [v("tout")], [v("tin")])],
+            3: [lambda: tt(v("s64"), v("tout", 0, 64), v("tout", 64, 128), op.add)],
+            4: [lambda: tt(v("s32"), v("s64", 0, 32), v("s64", 32, 64), op.add)],
+            5: [lambda: ts(v("fi"), v("s32"), 0.1, op.mult, -0.46, op.add)],
+            6: [lambda: ts(v("f10"), v("fi"), -10.0, op.mult)],
+            7: [lambda: tt(v("slot"), v("s32"), v("f10"), op.add)],
+            8: [lambda b=b: ts(v("zo", 24 * b, 24 * b + 24), v("slot", 0, 24), 16.0, op.mult, 4.0 * b, op.add) for b in (0, 1)]
+               + [lambda: ts(v("ho", 0, 8), v("ee", 0, 8), 4.0, op.mult, cr, op.add)],
+            9: [lambda b=b: ts(v("zo", 24 * b, 24 * b + 24), v("slot", 0, 24), 16.0, op.mult, 4.0 * b, op.add) for b in (2, 3)],
+        }
+        for t in range(TICKS):
+            if t == 0:
+                scan(v("rm"), ps(1, A), v("low"), -BIG, op.max, op.max)
+            else:
+                cp(v("msk"), ind(v("win"), v("o1", 8 * t, 8 * t + 8)))
+                scan(v("rm"), v("msk"), v("low"), -BIG, op.max, op.max)
+            act(v("junk", A * t, A * t + A), v("rm"), fn.Sign, bias=col("rm", A - 1), scale=-1.0, acc=col("ee", t))
+            for f in spare_v[t] + spare_s[t]:
+                f()
+            if t + 1 < TICKS:
+                ts(v("o5", 2 * t, 2 * t + 2), v("c5"), col("ee", t), op.add)
+                tt(v("cw", 32 * t + 32, 32 * t + 64), ind(v("tab"), v("o5", 2 * t, 2 * t + 2)), v("cw", 32 * t, 32 * t + 32), op.add)
+                scan(v("sc"), v("keep4"), v("cw", 32 * t + 32, 32 * t + 64), 0.0, op.mult, op.add)
+                cp(v("o1", 8 * t + 8, 8 * t + 16), v("sc", 3, 32, 4))
+
+        ts(v("ho", 8, TICKS), v("ee", 8, TICKS), 4.0, op.mult, cr, op.add)
+        cp(v("bm", 128, 160), ind(v("bh"), v("ho", 8, TICKS)))
+        if r == 1:
+            cp(v("ho2"), v("ee", 0, TICKS))
+            act(v("erow"), ind(v("num"), v("ho2")), fn.Copy)
+            act(v("lrow"), ind(v("erow"), v("zo", 0, 24)), fn.Copy)
+            dma("Y", "out", (T.ol[:, :], []), v("lrow", rows=slice(0, 128, 16)))
+        zt, H = "zt%d" % r, C // 2
+        banks = ((2, 3, 4, 5), (6, 7, 0, 1))
+        for h in range(2):
+            a = H * h
+            for b in range(4):
+                tt(v(zt, 4 * a + b, 4 * (a + H), 4), ind(v("bm"), v("zo", 24 * b + 12 * h, 24 * b + 12 * h + 12)),
+                   v("xh", C * b + a, C * b + a + H), op.add)
+            qz, sz = v("qz%d" % r, a, a + H), v("sz%d" % r, a, a + H)
+            quant(qz, sz, v(zt, 4 * a, 4 * (a + H)))
+            for b in range(4):
+                mm(banks[h][b], H, v("qw", 128 * b, 128 * b + 128), v("sw", 128 * b, 128 * b + 128), qz, sz)
+        Xn, Yn, qn, sn = xs[r + 1], ys[r + 1], "qx%d" % (r + 1), "sx%d" % (r + 1)
+        for h in range(2):
+            a = H * h
+            for b in range(4):
+                yn = v(Yn, C * b + a, C * b + a + H)
+                tt(yn, ps(banks[h][b], H), v(Y, C * b + a, C * b + a + H), op.add)
+                if (h, b) != (1, 3):
+                    act(v(Xn, 4 * a + b, 4 * (a + H), 4), yn, fn.Identity, scale=1.0 / 32)
+        for h in range(2):
+            a = H * h
+            quant(v(qn, a, a + H), v(sn, a, a + H), v(Xn, 4 * a, 4 * (a + H)))
+            if h == 0:
+                ts(v(Xn, 4 * H + 3, 4 * C, 4), v(Yn, 3 * C + H, 4 * C), 1.0 / 32, op.mult)
+            if r + 1 == len(STEPS):
+                mm(2 + h, H, v("qv"), v("sv"), v(qn, a, a + H), v(sn, a, a + H))
+                dma("Y", "out", (T.oc[:, 4 * a:4 * (a + H)], []), bytes_of(v(qn, a, a + H)))
+                if h == 0:
+                    act(v("yo", 0, H), ps(2, H), fn.Copy)
+                    dma("S", "out", (T.y[:, 0:H], []), v("yo", 0, H))
+                else:
+                    cp(v("yo", H, C), ps(3, H))
+                    dma("S", "out", (T.y[:, H:C], []), v("yo", H, C))
+    for k in range(4):
+        dma("Y", "out", (T.osc[4 * k:4 * k + 4, :], []), v("sx2", rows=slice(32 * k, 32 * k + 4)))
+    g.wait_ge(T.sem.sent, 2 * len(STEPS) * engines)
+    for sem in sorted(total):
+        wait("G", sem, total[sem])

@@ -8,8 +8,9 @@ F32, BF, I32, U16, X4, U8 = "float32", "bfloat16", "int32", "uint16", "float8_e4
 QUADS = [([0, 21, 22, 23], 384, 0), ([17, 18, 19, 20], 320, 384), ([13, 14, 15, 16], 256, 704),
          ([9, 10, 11, 12], 192, 960), ([5, 6, 7, 8], 128, 1152), ([1, 2, 3, 4], 128, 1280)]
 QCOLS, FIRSTV = 1408, 17
+LO = 256
 PARTS = {"s64": ("small", 0, 64), "s32": ("small", 64, 32), "f10": ("small", 96, 32), "slot": ("small", 128, 32),
-         "ho": ("hist", 0, TICKS), "ho2": ("hist", TICKS, TICKS), "sgn": ("sm", 0, C)}
+         "ho": ("hist", 0, TICKS), "ho2": ("hist", TICKS, TICKS), "sgn": ("ord", 0, C)}
 
 
 def _sb(n, d):
@@ -53,7 +54,7 @@ for _r in range(2):
 for _b in range(8):
     SCRATCH["ps%d" % _b] = ("psum", [128, 512], F32)
 
-SEMAPHORES = ["V", "S", "P", "G", "lx", "lu", "lv", "lwc", "lws", "tr0", "tr1", "out", "sent", "arr0", "arr1"]
+SEMAPHORES = ["V", "S", "P", "G", "lx", "lx2", "lu", "lv", "lwc", "lws", "tr0", "tr1", "out", "sent", "arr0", "arr1"]
 
 
 def rank_program(g, core, T, topo):
@@ -187,7 +188,8 @@ def rank_program(g, core, T, topo):
     group["out"] = 9 * 16
 
     dma("S", "lu", v("ut"), (T.u[:, :], []))
-    dma("Y", "lx", v("x0"), (T.x[:, :], []))
+    dma("Y", "lx", v("x0", 0, 4 * LO), (T.x[:, 0:4 * LO], []))
+    dma("Y", "lx2", v("x0", 4 * LO, 4 * C), (T.x[:, 4 * LO:4 * C], []))
     dma("Y", "lwc", bytes_of(v("qw")), (T.wc[:, :], []))
     dma("Y", "lws", v("sw"), (T.ws[:, :], []))
     dma("Y", "lv", v("vt"), (T.v[:, :], []))
@@ -207,13 +209,13 @@ def rank_program(g, core, T, topo):
     ts(col("pi", 4), col("pi", 0), 1, op.bitwise_and)
     ts(col("pi", 5), col("pi", 0), 2, op.bitwise_and)
     ts(col("pi", 6), col("pi", 0), 112, op.bitwise_and)
-    cp(v("pf", 0, 7), v("pi", 0, 7))
-    cq, ck, cr, b1, b2 = col("pf", 1), col("pf", 2), col("pf", 3), col("pf", 4), col("pf", 5)
     for ks, n, c0 in QUADS[:3]:
         fill(v("ct", 4 * (c0 + n - 48), 4 * (c0 + n)), 0.0)
-    ts(v("m16"), v("t16"), cq, op.is_equal)
+    cp(v("pf", 0, 7), v("pi", 0, 7))
+    cq, ck, cr, b1, b2 = col("pf", 1), col("pf", 2), col("pf", 3), col("pf", 4), col("pf", 5)
     for ks, n, c0 in QUADS[3:]:
         fill(v("ct", 4 * (c0 + 16 * ks[0]), 4 * (c0 + n)), 0.0)
+    ts(v("m16"), v("t16"), cq, op.is_equal)
     for b in range(4):
         issue("G", lambda b=b: g.affine_select(T.et[:, 512 * b:512 * b + 512], T.one[:, :], [[-1, 512]], op.is_equal, 0.0, b, 4),
               [v("et", 512 * b, 512 * b + 512)], [v("one")])
@@ -230,7 +232,7 @@ def rank_program(g, core, T, topo):
     ts(v("uko", 32, 40), v("g40", 32, 40), ck, op.add)
     act(col("acc", 0), ck, fn.Identity, scale=0.0)
     act(v("start"), v("t16"), fn.Identity, bias=-BIG, scale=2 * BIG)
-    act(v("keep16"), v("t16"), fn.Sign)
+    act(v("sgn"), v("t16"), fn.Sign, bias=cq, scale=-1.0)
     act(v("gate"), v("m16"), fn.Identity, bias=-BIG, scale=2 * BIG)
 
     def keeper(out, sign, tmp, run):
@@ -241,24 +243,24 @@ def rank_program(g, core, T, topo):
     def later_constants():
         act(col("col", 2), b1, fn.Identity, bias=EPS, scale=-2.0 * EPS)
         act(col("col", 3), b2, fn.Identity, bias=EPS, scale=-EPS)
+        act(col("col", 7), cr, fn.Identity, bias=112.0, scale=-16.0)
+        act(col("col", 6), cq, fn.Identity, bias=-63.5 / 128, scale=4.0)
         act(col("col", 4), ck, fn.Identity, bias=-1.0, scale=1.0 / 16)
         act(col("col", 5), ck, fn.Identity, bias=1.0, scale=-1.0 / 16)
-        act(col("col", 6), cq, fn.Identity, bias=-63.5 / 128, scale=4.0)
-        act(col("col", 7), cr, fn.Identity, bias=112.0, scale=-16.0)
-        act(v("keep4"), v("t4", 0, 32), fn.Sign)
         act(col("c5", 0), ck, fn.Identity, bias=col("col", 7), scale=256.0)
+        act(v("keep4"), v("t4", 0, 32), fn.Sign)
         act(v("cw", 0, 32, 4), v("g16"), fn.Identity, bias=col("col", 6), scale=4.0)
         act(col("c5", 1), col("c5", 0), fn.Identity, bias=-64.0)
 
+    ts(v("bt"), v("grp"), col("pf", 6), op.is_equal)
+    keeper("sel16", "sgn", "ex", 16)
     quant(v("qu"), v("su"), v("ut"))
+    quant(v("qb"), v("sb"), v("bt"))
     cp(words_of(v("qa")), ind(v("qu"), v("uaf"), dt.uint32))
     act(v("sa"), ind(v("su"), v("uaf")), fn.Copy)
-    ts(v("bt"), v("grp"), col("pf", 6), op.is_equal)
     cp(words_of(v("qk", 0, 320)), ind(v("qu"), v("uko", 0, 20), dt.uint32))
-    quant(v("qb"), v("sb"), v("bt"))
-    act(v("sgn"), v("t16"), fn.Sign, bias=cq, scale=-1.0)
     act(v("sk", 0, 320), ind(v("su"), v("uko", 0, 20)), fn.Copy)
-    keeper("sel16", "sgn", "ex", 16)
+    act(v("keep16"), v("t16"), fn.Sign)
     act(v("sk", 320, 640), ind(v("su"), v("uko", 20, 40)), fn.Copy)
 
     far = [T.cores[rank ^ s] for s in STEPS]
@@ -266,6 +268,8 @@ def rank_program(g, core, T, topo):
     for p in far[1:]:
         mask &= topo.mask(core, p)
     engines = bin(mask).count("1")
+    rest = [topo.mask(core, p) & ~mask for p in far]
+    second = [m if bin(m).count("1") == engines else mask for m in rest]
 
     def uk(j):
         return v("qk", 128 * j, 128 * j + 128), v("sk", 128 * j, 128 * j + 128)
@@ -277,24 +281,44 @@ def rank_program(g, core, T, topo):
         return v("ct", 4 * (c0 + a) + s, 4 * (c0 + b), 4)
 
     xs, ys = ["x0", "x1", "x2"], ["ya", "yb", "yc"]
-    quant(v("qx0"), v("sx0"), v("x0"))
+    cols = ((0, LO), (LO, C))
+
+    def scores(r, h):
+        a, b = cols[h]
+        qx, sx = v("qx%d" % r, a, b), v("sx%d" % r, a, b)
+        quant(qx, sx, v(xs[r], 4 * a, 4 * b))
+        if r < len(STEPS):
+            for bank in ((1, 0), (7,))[h]:
+                mm(bank, b - a, v("qa"), v("sa"), qx, sx)
+
+    def sv(a, b):
+        return v("ps1", a, b) if b <= LO else v("ps7", a - LO, b - LO)
+
+    scores(0, 0)
+    scores(0, 1)
+    cp(words_of(v("qk", 320, 640)), ind(v("qu"), v("uko", 20, 40), dt.uint32))
     for r in range(2):
         X, Y = xs[r], ys[r]
         qx, sx = v("qx%d" % r), v("sx%d" % r)
-        mm(1, C, v("qa"), v("sa"), qx, sx)
-        mm(0, C, v("qa"), v("sa"), qx, sx)
-        if r == 0:
-            cp(words_of(v("qk", 320, 640)), ind(v("qu"), v("uko", 20, 40), dt.uint32))
-        parts = ((208, 272), (0, 208), (272, C))
-        for a, b in parts:
-            tt(v("sm", a, b), v("ps1", a, b), v("gate", a, b), op.min)
-        for a, b in parts:
+
+        def keep1(a, b):
+            tt(v("sm", a, b), sv(a, b), v("gate", a, b), op.min)
+
+        def keep2(a, b):
             scan(v("sx", a, b), v("start", a, b), v("sm", a, b), -BIG, op.min, op.max)
+
+        keep1(192, LO)
+        keep1(0, 192)
+        keep1(LO, C)
+        keep2(192, LO)
+        keep2(0, 192)
+        keep2(LO, C)
         for j in range(4):
             mm(2 + j, C, uk(j)[0], uk(j)[1], qx, sx)
 
         def compare(k):
-            ts(cmp_view(k, 0, 16 * k), v("ps1", 0, 16 * k), col("sx", 16 * k + 15), op.is_lt)
+            for a, b in ((0, LO), (LO, 16 * k)):
+                ts(cmp_view(k, a, b), sv(a, b), col("sx", 16 * k + 15), op.is_lt)
 
         def count(k):
             e = 192 * (k - FIRSTV + 1)
@@ -308,78 +332,95 @@ def rank_program(g, core, T, topo):
         def sign(k):
             act(v("sg", 272 * k, 272 * k + 16 * k), v("ps0", 0, 16 * k), fn.Sign, bias=col("sx", 16 * k + 15), scale=-1.0)
 
-        sign(FIRSTV - 1)
-        for k in range(FIRSTV - 1, 0, -1):
-            if k > 1:
-                sign(k - 1)
+        turn = [15, 14, 13, 16] + list(range(12, 0, -1))
+        ahead = 0
+        for i, k in enumerate(turn):
+            while ahead < min(len(turn), i + (2 if k > 12 else 3 if k > 6 else 4)):
+                sign(turn[ahead])
+                ahead += 1
             act(cmp_view(k, 0, 16 * k), v("sg", 272 * k, 272 * k + 16 * k), fn.Relu, acc=col("acc", k))
-        if r == 0:
-            act(v("val"), v("num", 0, C), fn.Identity, bias=ck, scale=4.0)
-            act(v("sel2"), v("t4"), fn.Sign, bias=cr, scale=-1.0)
-            keeper("sel", "sel2", "osl", 4)
         act(v("cq"), ps(3), fn.Copy)
         act(v("cr"), ps(4), fn.Copy)
+        if r == 0:
+            act(v("sel2"), v("t4"), fn.Sign, bias=cr, scale=-1.0)
+            act(v("val"), v("num", 0, C), fn.Identity, bias=ck, scale=4.0)
+            keeper("sel", "sel2", "osl", 4)
+            later_constants()
 
-        tt(cmp_view(0, 0, C), ps(1), v("sx"), op.is_le)
+        tt(cmp_view(0, 0, LO), sv(0, LO), v("sx", 0, LO), op.is_le)
         compare(23)
+        tt(cmp_view(0, LO, C), sv(LO, C), v("sx", LO, C), op.is_le)
+        compare(22)
+        count(23)
+        scan(v("dr"), v("keep16"), cmp_view(0, 0, C), 0.0, op.mult, op.add)
+        compare(21)
+        count(22)
         if r == 0:
             ts(v("base", 0, FIRSTV), v("num", 0, 16 * FIRSTV, 16), cq, op.subtract, 14.625, op.add)
             ts(v("base", FIRSTV, 24), v("num", 16 * FIRSTV, C, 16), cq, op.subtract, 14.625 - 192, op.add)
-        scan(v("dr"), v("keep16"), cmp_view(0, 0, C), 0.0, op.mult, op.add)
-        compare(22)
-        count(23)
-        compare(21)
-        count(22)
-        tt(v("ra", 0, 24), v("base"), v("dr", 15, C, 16), op.subtract)
+        compare(20)
         count(21)
         quad(0)
-        compare(20)
+        tt(v("ra", 0, 24), v("base"), v("dr", 15, C, 16), op.subtract)
+        compare(19)
+        count(20)
         quad(2)
-        for k in (19, 18, 17):
-            compare(k)
-            count(k + 1)
+        compare(18)
+        count(19)
+        compare(17)
+        count(18)
+        quad(3)
         count(17)
         quad(1)
-        quad(3)
-        cp(v("acc", FIRSTV, 24), v("so", 191, None, 192))
         quad(4)
+        cp(v("acc", FIRSTV, 24), v("so", 191, None, 192))
         quad(5)
+        H = C // 2
+
+        def test(out, bank, other, how, h):
+            tt(v(out, H * h, H * h + H), v("ps%d" % bank, H * h, H * h + H), v(other, H * h, H * h + H), how)
+
         tt(v("ra", 24, 48), v("ra", 0, 24), v("acc"), op.subtract)
         if r == 0:
             quant(v("qe", 0, 256), v("se", 0, 256), v("et", 0, 1024))
         ts(v("ra", 48, 72), v("ra", 24, 48), 2.0 ** -13, op.mult)
+        test("d1", 2, "cq", op.subtract, 0)
         scan(v("ex"), ps(6), v("sel16"), 0.0, op.add, op.mult)
+        test("d1", 2, "cq", op.subtract, 1)
         tt(v("ra", 72, 96), v("ex", 15, C, 16), v("ra", 48, 72), op.add)
+        test("mrt", 5, "cr", op.max, 0)
         ts(v("rk"), v("ra", 72, 96), 8192.0, op.mult)
+        test("mrt", 5, "cr", op.max, 1)
+        act(v("y1"), v("d1"), fn.Sign, bias=col("col", 2))
         o = ind(v("ord"), v("rk"))
         issue("V", lambda o=o: g.vector.tensor_copy(o[0], T.val[:, :]), [v("ord")], [v("rk"), v("val")])
+        test("d2", 2, "mrt", op.subtract, 0)
         scan(v("osl"), v("ord", 0, 128), v("sel"), 0.0, op.add, op.mult)
+        test("d2", 2, "mrt", op.subtract, 1)
         ts(v("mo"), v("osl", 3, 128, 4), 8192.0, op.mult, -0.375, op.add)
+        ts(v("y2", 0, H), v("d2", 0, H), col("col", 3), op.add, 0.0, op.is_gt)
+        ts(v("y2", H, C), v("d2", H, C), col("col", 3), op.add, 0.0, op.is_gt)
         mt = "mt%d" % r
         act(v(mt, 256, 512), ind(v(X), v("mo", 16, 32)), fn.Copy)
         cp(v(mt, 0, 256), ind(v(X), v("mo", 0, 16)))
-        if r == 0:
-            later_constants()
+        tt(v("ind", 0, 128), v("y1", 0, 128), v("y2", 0, 128), op.is_equal)
         qm, sm, lq, ls = v("qm%d" % r), v("sm%d" % r), v("lq%d" % r), v("ls%d" % r)
         quant(qm, sm, v(mt))
         wait("G", "V", total["V"])
         rid, pid = topo.addr(far[r])[:2]
         arr = "arr%d" % r
         g.remote_dma(lq[0].bitcast(dt.uint8), qm[0].bitcast(dt.uint8), T.sem[arr], T.sem.sent, pid, rid, mask)
-        g.remote_dma(ls[0], sm[0], T.sem[arr], T.sem.sent, pid, rid, mask)
+        g.remote_dma(ls[0], sm[0], T.sem[arr], T.sem.sent, pid, rid, second[r])
 
-        tt(v("d1"), ps(2), v("cq"), op.subtract)
-        tt(v("mrt"), ps(5), v("cr"), op.max)
-        act(v("y1"), v("d1"), fn.Sign, bias=col("col", 2))
-        tt(v("d2"), ps(2), v("mrt"), op.subtract)
-        ts(v("y2"), v("d2"), col("col", 3), op.add, 0.0, op.is_gt)
-        tt(v("ind"), v("y1"), v("y2"), op.is_equal)
+        tt(v("ind", 128, C), v("y1", 128, C), v("y2", 128, C), op.is_equal)
         scan(v("cnt"), v("ind"), v("one", 0, C), col("col", 4), op.add, op.mult)
         ts(col("mu", 0), col("cnt", C - 1), col("col", 5), op.add)
+        tt(v("vk", 0, 128), v("cnt", 0, 128), v("ind", 0, 128), op.mult)
         ts(v("mrow"), ind(v("num"), col("mu", 0)), 1.0 / LIFE, op.mult)
-        tt(v("vk", 0, C), v("cnt"), v("ind"), op.mult)
+        tt(v("vk", 128, C), v("cnt", 128, C), v("ind", 128, C), op.mult)
         for k in range(4):
             act(v("tab", 256 * k + 112, 256 * k + 128), v("m16", 0, 16), fn.Identity, scale=col("mrow", k))
+        wait("Y", "sent", 2 * (r + 1) * engines)
         for h in range(2):
             for k in range(4):
                 dma("Y", "tr%d" % r, v("tin", 32 * k + 16 * h, 32 * k + 16 * h + 16),
@@ -388,7 +429,6 @@ def rank_program(g, core, T, topo):
         wait("P", arr, 2 * engines)
         mm(1, A, uk(4)[0], uk(4)[1], lq, ls)
         mm(0, A, uk(4)[0], uk(4)[1], lq, ls)
-        act(v("win", 0, 512, 4), ps(0, A), fn.Copy)
 
         def objects():
             if r == 0:
@@ -397,6 +437,7 @@ def rank_program(g, core, T, topo):
                 mm(2 + b, A, v("qe", 128 * b, 128 * b + 128), v("se", 128 * b, 128 * b + 128), lq, ls)
 
         spare_s = {t: [] for t in range(TICKS)}
+        spare_s[0].append(lambda: act(v("win", 0, 512, 4), ps(0, A), fn.Copy))
         for b in range(4):
             spare_s[b + 1].append(lambda b=b: act(v("bh", b, 512, 4), ps(2 + b, A), fn.Identity, scale=0.5))
             if r == 0:
@@ -406,15 +447,15 @@ def rank_program(g, core, T, topo):
         spare_v = {
             0: [objects],
             1: [lambda: quant(v("qv"), v("sv"), v("vt"))] if r == 0 else [],
-            2: [lambda: issue("V", lambda: g.vector.transpose(T.tout[:, :], T.tin[:, :]), [v("tout")], [v("tin")])],
-            3: [lambda: tt(v("s64"), v("tout", 0, 64), v("tout", 64, 128), op.add)],
-            4: [lambda: tt(v("s32"), v("s64", 0, 32), v("s64", 32, 64), op.add)],
-            5: [lambda: ts(v("fi"), v("s32"), 0.1, op.mult, -0.46, op.add)],
-            6: [lambda: ts(v("f10"), v("fi"), -10.0, op.mult)],
-            7: [lambda: tt(v("slot"), v("s32"), v("f10"), op.add)],
-            8: [lambda b=b: ts(v("zo", 24 * b, 24 * b + 24), v("slot", 0, 24), 16.0, op.mult, 4.0 * b, op.add) for b in (0, 1)]
-               + [lambda: ts(v("ho", 0, 8), v("ee", 0, 8), 4.0, op.mult, cr, op.add)],
-            9: [lambda b=b: ts(v("zo", 24 * b, 24 * b + 24), v("slot", 0, 24), 16.0, op.mult, 4.0 * b, op.add) for b in (2, 3)],
+            2: [],
+            3: [lambda: issue("V", lambda: g.vector.transpose(T.tout[:, :], T.tin[:, :]), [v("tout")], [v("tin")])],
+            4: [lambda: tt(v("s64"), v("tout", 0, 64), v("tout", 64, 128), op.add)],
+            5: [lambda: tt(v("s32"), v("s64", 0, 32), v("s64", 32, 64), op.add)],
+            6: [lambda: ts(v("fi"), v("s32"), 0.1, op.mult, -0.46, op.add)],
+            7: [lambda: ts(v("f10"), v("fi"), -10.0, op.mult)],
+            8: [lambda: tt(v("slot"), v("s32"), v("f10"), op.add),
+                lambda: ts(v("ho", 0, 8), v("ee", 0, 8), 4.0, op.mult, cr, op.add)],
+            9: [lambda b=b: ts(v("zo", 24 * b, 24 * b + 24), v("slot", 0, 24), 16.0, op.mult, 4.0 * b, op.add) for b in range(4)],
         }
         for t in range(TICKS):
             if t == 0:
@@ -432,45 +473,66 @@ def rank_program(g, core, T, topo):
                 cp(v("o1", 8 * t + 8, 8 * t + 16), v("sc", 3, 32, 4))
 
         ts(v("ho", 8, TICKS), v("ee", 8, TICKS), 4.0, op.mult, cr, op.add)
-        cp(v("bm", 128, 160), ind(v("bh"), v("ho", 8, TICKS)))
         if r == 1:
             cp(v("ho2"), v("ee", 0, TICKS))
+        cp(v("bm", 128, 160), ind(v("bh"), v("ho", 8, TICKS)))
+        if r == 1:
             act(v("erow"), ind(v("num"), v("ho2")), fn.Copy)
             act(v("lrow"), ind(v("erow"), v("zo", 0, 24)), fn.Copy)
             dma("Y", "out", (T.ol[:, :], []), v("lrow", rows=slice(0, 128, 16)))
-        zt, H = "zt%d" % r, C // 2
+        zt = "zt%d" % r
         banks = ((2, 3, 4, 5), (6, 7, 0, 1))
-        for h in range(2):
-            a = H * h
-            for b in range(4):
-                tt(v(zt, 4 * a + b, 4 * (a + H), 4), ind(v("bm"), v("zo", 24 * b + 12 * h, 24 * b + 12 * h + 12)),
-                   v("xh", C * b + a, C * b + a + H), op.add)
-            qz, sz = v("qz%d" % r, a, a + H), v("sz%d" % r, a, a + H)
-            quant(qz, sz, v(zt, 4 * a, 4 * (a + H)))
-            for b in range(4):
-                mm(banks[h][b], H, v("qw", 128 * b, 128 * b + 128), v("sw", 128 * b, 128 * b + 128), qz, sz)
         Xn, Yn, qn, sn = xs[r + 1], ys[r + 1], "qx%d" % (r + 1), "sx%d" % (r + 1)
-        for h in range(2):
-            a = H * h
+
+        def take(h, b):
+            a, e = cols[h]
+            tt(v(zt, 4 * a + b, 4 * e, 4), ind(v("bm"), v("zo", 24 * b + a // 16, 24 * b + e // 16)),
+               v("xh", C * b + a, C * b + e), op.add)
+
+        def layer(h):
+            a, e = cols[h]
+            qz, sz = v("qz%d" % r, a, e), v("sz%d" % r, a, e)
+            quant(qz, sz, v(zt, 4 * a, 4 * e))
             for b in range(4):
-                yn = v(Yn, C * b + a, C * b + a + H)
-                tt(yn, ps(banks[h][b], H), v(Y, C * b + a, C * b + a + H), op.add)
-                if (h, b) != (1, 3):
-                    act(v(Xn, 4 * a + b, 4 * (a + H), 4), yn, fn.Identity, scale=1.0 / 32)
+                mm(banks[h][b], e - a, v("qw", 128 * b, 128 * b + 128), v("sw", 128 * b, 128 * b + 128), qz, sz)
+
+        def renew(h, b):
+            a, e = cols[h]
+            yn = v(Yn, C * b + a, C * b + e)
+            tt(yn, ps(banks[h][b], e - a), v(Y, C * b + a, C * b + e), op.add)
+            if b < 3 - h:
+                act(v(Xn, 4 * a + b, 4 * e, 4), yn, fn.Identity, scale=1.0 / 32)
+
+        def shrink(h, b):
+            a, e = cols[h]
+            ts(v(Xn, 4 * a + b, 4 * e, 4), v(Yn, C * b + a, C * b + e), 1.0 / 32, op.mult)
+
+        for b in range(4):
+            take(0, b)
+        take(1, 0)
+        layer(0)
+        for b in range(1, 4):
+            take(1, b)
+        renew(0, 0)
+        layer(1)
+        for b in range(1, 4):
+            renew(0, b)
+        renew(1, 0)
+        renew(1, 1)
+        shrink(0, 3)
+        renew(1, 2)
+        renew(1, 3)
         for h in range(2):
-            a = H * h
-            quant(v(qn, a, a + H), v(sn, a, a + H), v(Xn, 4 * a, 4 * (a + H)))
+            a, e = cols[h]
+            scores(r + 1, h)
             if h == 0:
-                ts(v(Xn, 4 * H + 3, 4 * C, 4), v(Yn, 3 * C + H, 4 * C), 1.0 / 32, op.mult)
+                shrink(1, 2)
+                shrink(1, 3)
             if r + 1 == len(STEPS):
-                mm(2 + h, H, v("qv"), v("sv"), v(qn, a, a + H), v(sn, a, a + H))
-                dma("Y", "out", (T.oc[:, 4 * a:4 * (a + H)], []), bytes_of(v(qn, a, a + H)))
-                if h == 0:
-                    act(v("yo", 0, H), ps(2, H), fn.Copy)
-                    dma("S", "out", (T.y[:, 0:H], []), v("yo", 0, H))
-                else:
-                    cp(v("yo", H, C), ps(3, H))
-                    dma("S", "out", (T.y[:, H:C], []), v("yo", H, C))
+                mm(2 + h, e - a, v("qv"), v("sv"), v(qn, a, e), v(sn, a, e))
+                dma("Y", "out", (T.oc[:, 4 * a:4 * e], []), bytes_of(v(qn, a, e)))
+                act(v("yo", a, e), ps(2 + h, e - a), fn.Copy)
+                dma("S", "out", (T.y[:, a:e], []), v("yo", a, e))
     for k in range(4):
         dma("Y", "out", (T.osc[4 * k:4 * k + 4, :], []), v("sx2", rows=slice(32 * k, 32 * k + 4)))
     g.wait_ge(T.sem.sent, 2 * len(STEPS) * engines)

@@ -1,16 +1,38 @@
-from concourse.mybir import dt, AluOpType, ActivationFunctionType
+from concourse.mybir import dt, AluOpType, ActivationFunctionType, AxisListType
 
 C, A, LIFE, TICKS = 384, 128, 128, 10
 STEPS = [1, 2]
 BIG = 1e29
 EPS = 2.0 ** -100
+UNIT = 512.0
 F32, BF, I32, U16, X4, U8 = "float32", "bfloat16", "int32", "uint16", "float8_e4m3fn_x4", "uint8"
 QUADS = [([0, 21, 22, 23], 384, 0), ([17, 18, 19, 20], 320, 384), ([13, 14, 15, 16], 256, 704),
          ([9, 10, 11, 12], 192, 960), ([5, 6, 7, 8], 128, 1152), ([1, 2, 3, 4], 128, 1280)]
-QCOLS, FIRSTV = 1408, 17
-LO = 256
+QCOLS = 1408
+CUTS = [(0, 128), (128, 256), (256, C)]
+VSPANS = [[(14, 16), (19, 24)], [(13, 16), (20, 24)]]
+SBLOCKS = [[(0, [7, 6, 5]), (1, [13, 12, 11, 10]), (2, [16, 17, 18]), (1, [9, 8, 4, 3, 2, 1])],
+           [(0, [7, 6, 5]), (1, [12, 11, 10, 9]), (2, [16, 17, 18, 19]), (1, [8, 4, 3, 2, 1])]]
+SG = 16 * 21
+FETCH = (2, 3, 6, 7, 9, 10, 11)
+OWN = [(3, 7, 8, 9, 10, 11), (3, 7, 11)]
+PLAN0 = ("pick0 scores0 base0 pick1 scores1 mask0 pick2 keep0 signs0 scores2 mask1 inner0 keep1 signs1 pick3 "
+         "compare15 mask2 compare14 inner1 keep2 signs2 signs3 count14 sum0 count15 sum1 "
+         "compare23 compare22 inner2 tastes0 compare21 sum2 compare20 count23 quad0 compare19 count22 "
+         "quad2 count21 quad1 count20 quad3 count19 quad4 places0 sums0 sums1 quad5")
+TAKE = ("take0 take1 take4 take2 take3 take5 layer0 take6 take7 take8 layer1 %s renew0 renew1 take9 renew2 renew3 "
+        "take10 take11 shrink3 renew4 ")
+PLAN1 = TAKE % "" + (
+    "scores0 renew5 layer2 renew6 renew7 mask0 shrink7 keep0 signs0 scores1 renew8 inner0 renew9 renew10 renew11 "
+    "shrink8 mask1 shrink9 shrink10 shrink11 keep1 signs1 scores2 inner1 compare15 compare13 sum1 mask2 compare14 sum0 "
+    "keep2 signs2 signs3 tastes0 count15 count14 count13 compare23 compare22 inner2 compare21 sum2 compare20 quad0 "
+    "count23 quad2 count22 quad3 count21 quad1 count20 quad4 places0 sums0 sums1 quad5")
+PLAN2 = TAKE % "lists0" + (
+    "codes0 renew5 layer2 renew6 renew7 store0 shrink7 renew8 codes1 renew9 renew10 renew11 store1 shrink11 codes2 "
+    "lists1 store2")
 PARTS = {"s64": ("small", 0, 64), "s32": ("small", 64, 32), "f10": ("small", 96, 32), "slot": ("small", 128, 32),
-         "ho": ("hist", 0, TICKS), "ho2": ("hist", TICKS, TICKS), "sgn": ("ord", 0, C)}
+         "ho": ("hist", 0, TICKS), "ho2": ("hist", TICKS, TICKS),
+         "sgr": ("wts", 0, 16), "wa": ("wts", 16, 16), "wb": ("wts", 32, 16)}
 
 
 def _sb(n, d):
@@ -24,28 +46,29 @@ SCRATCH = {
     "qa": _sb(128, X4), "sa": _sb(128, U8), "qk": _sb(640, X4), "sk": _sb(640, U8),
     "qw": _sb(512, X4), "sw": _sb(512, U8),
     "one": _sb(512, BF), "et": _sb(2048, BF), "qe": _sb(512, X4), "se": _sb(512, U8),
-    "grp": _sb(512, BF), "bt": _sb(512, BF), "qb": _sb(128, X4), "sb": _sb(128, U8),
+    "bt": _sb(512, BF), "qb": _sb(128, X4), "sb": _sb(128, U8),
     "pi": _sb(16, I32), "pf": _sb(16, F32), "col": _sb(16, F32),
-    "g16": _sb(8, F32), "t16": _sb(C, F32), "t4": _sb(128, F32), "num": _sb(400, F32),
+    "g16": _sb(8, F32), "t16": _sb(C, BF), "t4": _sb(128, F32), "num": _sb(400, F32),
     "uaf": _sb(8, U16), "g40": _sb(40, F32), "uko": _sb(40, U16),
-    "m16": _sb(C, F32), "gate": _sb(C, F32), "start": _sb(C, F32), "keep16": _sb(C, BF),
-    "sel16": _sb(C, F32), "base": _sb(24, F32),
-    "val": _sb(C, F32), "sel": _sb(128, F32), "sel2": _sb(128, F32), "keep4": _sb(32, F32),
-    "c5": _sb(2, F32), "low": _sb(128, F32),
+    "gate": _sb(C, BF), "start": _sb(C, F32), "keep16": _sb(C, BF),
+    "sel16": _sb(C, BF), "base": _sb(48, F32),
+    "val": _sb(C, F32), "sel": _sb(128, F32), "sel2": _sb(128, F32),
+    "c5": _sb(4, F32), "low": _sb(128, F32), "wts": _sb(48, F32),
     "sm": _sb(C, F32), "sx": _sb(C, F32), "dr": _sb(C, BF), "ct": _sb(4 * QCOLS, BF), "cc": _sb(QCOLS, X4),
-    "cs": _sb(QCOLS, U8), "so": _sb((24 - FIRSTV) * 192, BF), "sg": _sb(FIRSTV * 272, BF), "junk": _sb(A * TICKS, BF),
+    "cs": _sb(QCOLS, U8), "so": _sb(7 * 192, BF), "sg": _sb(SG * SG // 16, BF),
     "acc": _sb(24, F32), "ra": _sb(96, F32), "ex": _sb(C, F32), "rk": _sb(24, U16),
     "ord": _sb(C, F32), "osl": _sb(128, F32), "mo": _sb(32, U16),
     "cq": _sb(C, F32), "cr": _sb(C, F32), "mrt": _sb(C, F32), "d1": _sb(C, BF), "d2": _sb(C, BF),
     "y1": _sb(C, BF), "y2": _sb(C, BF), "ind": _sb(C, BF), "cnt": _sb(C, F32), "vk": _sb(512, F32),
-    "mu": _sb(2, U16), "mrow": _sb(16, F32), "tab": _sb(1024, F32),
+    "mu": _sb(2, U16), "mrow": _sb(32, F32),
     "tin": _sb(128, F32), "tout": _sb(128, F32), "small": _sb(160, F32), "fi": _sb(32, I32), "zo": _sb(96, U16),
-    "win": _sb(512, F32), "msk": _sb(128, F32), "rm": _sb(128, F32), "ee": _sb(16, F32), "o5": _sb(2 * TICKS, U16),
-    "cw": _sb(32 * TICKS, F32), "sc": _sb(32, F32), "o1": _sb(8 * TICKS, U16),
+    "msk": _sb(144, F32), "alive": _sb(144, F32), "rm": _sb(128, F32), "step": _sb(144, F32), "ee": _sb(16, F32),
+    "o5": _sb(4 * TICKS, U16), "ww": _sb(16 * TICKS, F32), "wt": _sb(48, F32), "sc": _sb(TICKS, F32),
+    "o1": _sb(2 * TICKS, U16),
     "bh": _sb(512, F32), "hist": _sb(2 * TICKS, U16), "bm": _sb(160, F32), "erow": _sb(160, F32),
     "lrow": _sb(C, F32),
-    "xh": _sb(4 * C, BF), "ya": _sb(4 * C, BF), "yb": _sb(4 * C, BF), "yc": _sb(4 * C, BF), "yo": _sb(C, F32),
-    "qx2": _sb(C, X4), "sx2": _sb(C, U8),
+    "xh": _sb(4 * C, BF), "got": _sb(4 * C, BF), "ya": _sb(4 * C, BF), "yb": _sb(4 * C, BF), "yc": _sb(4 * C, BF),
+    "yo": _sb(C, F32), "qx2": _sb(C, X4), "sx2": _sb(C, U8),
 }
 for _r in range(2):
     SCRATCH.update({"qx%d" % _r: _sb(C, X4), "sx%d" % _r: _sb(C, U8), "mt%d" % _r: _sb(512, BF),
@@ -54,7 +77,7 @@ for _r in range(2):
 for _b in range(8):
     SCRATCH["ps%d" % _b] = ("psum", [128, 512], F32)
 
-SEMAPHORES = ["V", "S", "P", "G", "lx", "lx2", "lu", "lv", "lwc", "lws", "tr0", "tr1", "out", "sent", "arr0", "arr1"]
+SEMAPHORES = ["V", "S", "P", "G", "lx0", "lx1", "lx2", "lu", "lv", "lwc", "lws", "tr0", "tr1", "out", "sent", "arr0", "arr1"]
 
 
 def rank_program(g, core, T, topo):
@@ -140,8 +163,14 @@ def rank_program(g, core, T, topo):
     def cp(o, i):
         issue("V", lambda: g.vector.tensor_copy(o[0], i[0]), [o], [i])
 
+    def scatter(window, offsets, i):
+        issue("V", lambda: g.vector.tensor_copy(window[0].indirect(offsets[0]), i[0]), [window], [offsets, i])
+
     def scan(o, a, b, init, o0, o1):
         issue("V", lambda: g.vector.tensor_tensor_scan(o[0], a[0], b[0], ap(init), o0, o1), [o], [a, b, init])
+
+    def minus_sum(o, i):
+        issue("V", lambda: g.vector.tensor_reduce(o[0], i[0], AxisListType.X, op.add, negate=True), [o], [i])
 
     def fill(o, c):
         issue("V", lambda: g.vector.memset(o[0], c), [o], [])
@@ -185,11 +214,13 @@ def rank_program(g, core, T, topo):
         return (x[0].bitcast(dt.uint32), x[1])
 
     group["tr0"] = group["tr1"] = 8 * 16
-    group["out"] = 9 * 16
+    group["out"] = 11 * 16
+    H = C // 2
 
     dma("S", "lu", v("ut"), (T.u[:, :], []))
-    dma("Y", "lx", v("x0", 0, 4 * LO), (T.x[:, 0:4 * LO], []))
-    dma("Y", "lx2", v("x0", 4 * LO, 4 * C), (T.x[:, 4 * LO:4 * C], []))
+    for h, (a, b) in enumerate(CUTS):
+        dma("Y", "lx%d" % h, v("x0", 4 * a, 4 * b), (T.x[:, 4 * a:4 * b], []))
+    wait("Y", "lx2", 16)
     dma("Y", "lwc", bytes_of(v("qw")), (T.wc[:, :], []))
     dma("Y", "lws", v("sw"), (T.ws[:, :], []))
     dma("Y", "lv", v("vt"), (T.v[:, :], []))
@@ -198,10 +229,15 @@ def rank_program(g, core, T, topo):
     iota(col("pi", 0), [[0, 1]], 0, 1, small=False)
     iota(v("t16"), [[0, 24], [1, 16]])
     iota(v("g40"), [[1, 5], [16, 8]], 4)
-    iota(v("grp"), [[16, 8], [0, 64]])
-    iota(v("t4"), [[0, 32], [1, 4]])
     iota(v("num"), [[1, 400]])
+    iota(v("t4"), [[0, 32], [1, 4]])
+
+    def blank(quads):
+        for ks, n, c0 in quads:
+            fill(v("ct", 4 * (c0 + 16 * min(k for k in ks if k)), 4 * (c0 + n)), 0.0)
+
     fill(v("one"), 1.0)
+    blank(QUADS[:2])
     cp(v("uaf"), v("g16"))
     ts(col("pi", 1), col("pi", 0), 15, op.bitwise_and)
     ts(col("pi", 2), col("pi", 0), 3, op.bitwise_and)
@@ -209,67 +245,77 @@ def rank_program(g, core, T, topo):
     ts(col("pi", 4), col("pi", 0), 1, op.bitwise_and)
     ts(col("pi", 5), col("pi", 0), 2, op.bitwise_and)
     ts(col("pi", 6), col("pi", 0), 112, op.bitwise_and)
-    for ks, n, c0 in QUADS[:3]:
-        fill(v("ct", 4 * (c0 + n - 48), 4 * (c0 + n)), 0.0)
+    blank(QUADS[2:5])
     cp(v("pf", 0, 7), v("pi", 0, 7))
+    blank(QUADS[5:])
     cq, ck, cr, b1, b2 = col("pf", 1), col("pf", 2), col("pf", 3), col("pf", 4), col("pf", 5)
-    for ks, n, c0 in QUADS[3:]:
-        fill(v("ct", 4 * (c0 + 16 * ks[0]), 4 * (c0 + n)), 0.0)
-    ts(v("m16"), v("t16"), cq, op.is_equal)
+    ts(v("pf", 8, 16), v("g16"), col("pf", 6), op.is_equal)
+    ts(v("gate"), v("t16"), cq, op.not_equal, -2 * BIG, op.mult)
+    for j in range(8):
+        act(v("bt", 64 * j, 64 * j + 64), v("one", 0, 64), fn.Identity, scale=col("pf", 8 + j))
     for b in range(4):
         issue("G", lambda b=b: g.affine_select(T.et[:, 512 * b:512 * b + 512], T.one[:, :], [[-1, 512]], op.is_equal, 0.0, b, 4),
               [v("et", 512 * b, 512 * b + 512)], [v("one")])
-    for name, n in (("win", 512), ("low", 128)):
+    for name, n in (("msk", 144), ("low", 128)):
         issue("G", lambda name=name, n=n: g.affine_select(T[name][:, :], T.one[:, 0:n], [[0, n]], op.is_equal, -BIG, 1, 0),
               [v(name)], [v("one")])
-    iota(v("tab"), [[0, 1024]])
+    iota(v("step"), [[0, 144]], 1)
+    iota(v("alive", A, 144), [[0, 16]])
     iota(v("vk", C, 512), [[0, 128]])
-    iota(v("cw", 0, 32), [[0, 32]])
+    act(col("acc", 0), ck, fn.Identity, scale=0.0)
+    act(v("start"), v("t16"), fn.Identity, bias=-BIG, scale=2 * BIG)
+    act(v("keep16"), v("t16"), fn.Sign)
+
+    def later_constants():
+        act(v("sel2"), v("t4"), fn.Sign, bias=cr, scale=-1.0)
+        act(v("val"), v("num", 0, C), fn.Identity, bias=ck, scale=4.0)
+        act(v("osl"), v("sel2"), fn.Abs, bias=-0.5, scale=-8192.0)
+        act(col("col", 2), b1, fn.Identity, bias=EPS, scale=-2.0 * EPS)
+        act(col("col", 3), b2, fn.Identity, bias=EPS, scale=-EPS)
+        act(col("col", 7), cq, fn.Identity, bias=float(A))
+        act(col("col", 6), cr, fn.Relu, bias=-1000.0, scale=1000.0)
+        act(v("sel"), v("osl"), fn.Relu, bias=8192.5, scale=-1.0)
+        act(col("col", 4), ck, fn.Identity, bias=-1.0, scale=1.0 / 16)
+        act(col("col", 5), ck, fn.Identity, bias=1.0, scale=-1.0 / 16)
+        act(v("c5", 0, 2), v("one", 0, 2), fn.Identity, bias=col("col", 6), scale=cr)
+        act(v("c5", 2, 4), v("one", 0, 2), fn.Identity, bias=col("col", 6), scale=0.0)
+        act(v("sel", 3, None, 4), v("sel2", 3, None, 4), fn.Identity, bias=2.0 ** -13, scale=2.0 ** -13 - 2.0 ** -26)
+
+    def weights():
+        fill(v("sgr", 0, 4), UNIT)
+        fill(v("sgr", 4, 8), -UNIT)
+        fill(v("sgr", 8, 16), 0.0)
+        ts(v("wt", 0, 16), v("t4", 0, 16), ck, op.is_ge)
+        return [lambda: tt(v("wa"), v("wt", 0, 16), v("sgr"), op.mult),
+                lambda: tt(v("wt", 16, 32), v("wa"), v("sgr"), op.subtract),
+                lambda: ts(v("wb"), v("wt", 16, 32), 4096.0, op.mult),
+                lambda: ts(col("wb", 8), cr, -2.0 ** 30, op.mult, (0.5 - LIFE) * UNIT, op.add)]
+
+    ts(v("d1"), v("t16"), cq, op.is_equal, 8192.0, op.mult)
+    ts(v("d2"), v("t16"), cq, op.is_gt)
     ts(v("uko", 0, 8), v("g40", 0, 8), ck, op.add)
     ts(v("uko", 8, 16), v("g40", 8, 16), b2, op.add, b1, op.subtract)
     ts(v("uko", 16, 24), v("g40", 16, 24), b1, op.add, b2, op.subtract)
     ts(v("uko", 24, 32), v("g40", 24, 32), ck, op.subtract)
+    tt(v("sel16"), v("d1"), v("d2"), op.add)
     ts(v("uko", 32, 40), v("g40", 32, 40), ck, op.add)
-    act(col("acc", 0), ck, fn.Identity, scale=0.0)
-    act(v("start"), v("t16"), fn.Identity, bias=-BIG, scale=2 * BIG)
-    act(v("sgn"), v("t16"), fn.Sign, bias=cq, scale=-1.0)
-    act(v("gate"), v("m16"), fn.Identity, bias=-BIG, scale=2 * BIG)
-
-    def keeper(out, sign, tmp, run):
-        act(v(tmp), v(sign), fn.Abs, bias=-0.5, scale=-8192.0)
-        act(v(out), v(tmp), fn.Relu, bias=8192.5, scale=-1.0)
-        act(v(out, run - 1, None, run), v(sign, run - 1, None, run), fn.Identity, bias=2.0 ** -13, scale=2.0 ** -13 - 2.0 ** -26)
-
-    def later_constants():
-        act(col("col", 2), b1, fn.Identity, bias=EPS, scale=-2.0 * EPS)
-        act(col("col", 3), b2, fn.Identity, bias=EPS, scale=-EPS)
-        act(col("col", 7), cr, fn.Identity, bias=112.0, scale=-16.0)
-        act(col("col", 6), cq, fn.Identity, bias=-63.5 / 128, scale=4.0)
-        act(col("col", 4), ck, fn.Identity, bias=-1.0, scale=1.0 / 16)
-        act(col("col", 5), ck, fn.Identity, bias=1.0, scale=-1.0 / 16)
-        act(col("c5", 0), ck, fn.Identity, bias=col("col", 7), scale=256.0)
-        act(v("keep4"), v("t4", 0, 32), fn.Sign)
-        act(v("cw", 0, 32, 4), v("g16"), fn.Identity, bias=col("col", 6), scale=4.0)
-        act(col("c5", 1), col("c5", 0), fn.Identity, bias=-64.0)
-
-    ts(v("bt"), v("grp"), col("pf", 6), op.is_equal)
-    keeper("sel16", "sgn", "ex", 16)
     quant(v("qu"), v("su"), v("ut"))
     quant(v("qb"), v("sb"), v("bt"))
+    ts(v("sel16", 15, C, 16), v("sel16", 15, C, 16), 2.0 ** -26, op.mult)
     cp(words_of(v("qa")), ind(v("qu"), v("uaf"), dt.uint32))
     act(v("sa"), ind(v("su"), v("uaf")), fn.Copy)
-    cp(words_of(v("qk", 0, 320)), ind(v("qu"), v("uko", 0, 20), dt.uint32))
-    act(v("sk", 0, 320), ind(v("su"), v("uko", 0, 20)), fn.Copy)
-    act(v("keep16"), v("t16"), fn.Sign)
-    act(v("sk", 320, 640), ind(v("su"), v("uko", 20, 40)), fn.Copy)
+
+    def pick(j):
+        cp(words_of(v("qk", 128 * j, 128 * j + 128)), ind(v("qu"), v("uko", 8 * j, 8 * j + 8), dt.uint32))
+
+    def pick_scales(j):
+        act(v("sk", 128 * j, 128 * j + 128), ind(v("su"), v("uko", 8 * j, 8 * j + 8)), fn.Copy)
+
+    for j in range(4):
+        pick_scales(j)
 
     far = [T.cores[rank ^ s] for s in STEPS]
-    mask = topo.mask(core, far[0])
-    for p in far[1:]:
-        mask &= topo.mask(core, p)
-    engines = bin(mask).count("1")
-    rest = [topo.mask(core, p) & ~mask for p in far]
-    second = [m if bin(m).count("1") == engines else mask for m in rest]
+    sent = [2 * sum(len(topo.engines(core, p)) for p in far[:r + 1]) for r in range(len(far))]
 
     def uk(j):
         return v("qk", 128 * j, 128 * j + 128), v("sk", 128 * j, 128 * j + 128)
@@ -281,260 +327,282 @@ def rank_program(g, core, T, topo):
         return v("ct", 4 * (c0 + a) + s, 4 * (c0 + b), 4)
 
     xs, ys = ["x0", "x1", "x2"], ["ya", "yb", "yc"]
-    cols = ((0, LO), (LO, C))
+    VS, SS, SUMS, TASTE = (4, 2, 6), (5, 3, 7), 0, (1, 4, 5, 2)
+    LAYER, LAST = ((4, 5, 6, 7), (0, 1, 2, 3), (6, 7, 0, 1)), (4, 5, 2)
+
+    def part(h):
+        return v("ps%d" % VS[h], *CUTS[h])
 
     def scores(r, h):
-        a, b = cols[h]
-        qx, sx = v("qx%d" % r, a, b), v("sx%d" % r, a, b)
-        quant(qx, sx, v(xs[r], 4 * a, 4 * b))
-        if r < len(STEPS):
-            for bank in ((1, 0), (7,))[h]:
-                mm(bank, b - a, v("qa"), v("sa"), qx, sx)
+        a, b = CUTS[h]
+        quant(v("qx%d" % r, a, b), v("sx%d" % r, a, b), v(xs[r], 4 * a, 4 * b))
+        if h == 2:
+            mm(SUMS, b - a, v("qa"), v("sa"), v("qx%d" % r, a, b), v("sx%d" % r, a, b))
+        for bank in (VS[h], SS[h]):
+            mm(bank, b, v("qa"), v("sa"), v("qx%d" % r, 0, b), v("sx%d" % r, 0, b))
 
-    def sv(a, b):
-        return v("ps1", a, b) if b <= LO else v("ps7", a - LO, b - LO)
+    def mask(h):
+        tt(v("sm", *CUTS[h]), ps(SUMS, A) if h == 2 else part(h), v("gate", *CUTS[h]), op.add)
 
-    scores(0, 0)
-    scores(0, 1)
-    cp(words_of(v("qk", 320, 640)), ind(v("qu"), v("uko", 20, 40), dt.uint32))
+    def keep(h):
+        scan(v("sx", *CUTS[h]), v("start", *CUTS[h]), v("sm", *CUTS[h]), -BIG, op.min, op.max)
+
+    def inner(h):
+        tt(cmp_view(0, *CUTS[h]), part(h), v("sx", *CUTS[h]), op.is_le)
+
+    def inner_sum(h):
+        scan(v("dr", *CUTS[h]), v("keep16", *CUTS[h]), cmp_view(0, *CUTS[h]), 0.0, op.mult, op.add)
+
+    def compare(k):
+        ts(cmp_view(k, 0, 16 * k), ps(VS[k // 8], 16 * k), col("sx", 16 * k + 15), op.is_lt)
+
+    def end(r, k):
+        return 192 * (1 + [j for a, b in VSPANS[r] for j in range(a, b)].index(k))
+
+    def count(r, k):
+        e = end(r, k)
+        scan(v("so", e - 8 * k, e), cmp_view(k, 0, 8 * k), cmp_view(k, 8 * k, 16 * k), -192.0, op.add, op.add)
+
+    def sums(r, j):
+        a, b = VSPANS[r][j]
+        cp(v("acc", a, b), v("so", end(r, a) - 1, end(r, b - 1), 192))
+
+    done = []
+
+    def quad(i):
+        ks, n, c0 = QUADS[i]
+        quant(v("cc", c0, c0 + n), v("cs", c0, c0 + n), v("ct", 4 * c0, 4 * (c0 + n)))
+        done.append(i)
+        mm(SUMS, n, v("qb"), v("sb"), v("cc", c0, c0 + n), v("cs", c0, c0 + n),
+           len(done) % len(QUADS) == 1, len(done) % len(QUADS) == 0)
+
+    def signs(h, turn):
+        n = 0
+        for i, k in enumerate(turn):
+            while n < min(len(turn), i + (2 if k > 12 else 3 if k > 7 else 4)):
+                j = turn[n]
+                act(v("sg", SG * j, SG * j + 16 * j), ps(SS[h], 16 * j), fn.Sign, bias=col("sx", 16 * j + 15), scale=-1.0)
+                n += 1
+            act(cmp_view(k, 0, 16 * k), v("sg", SG * k, SG * k + 16 * k), fn.Relu, acc=col("acc", k))
+
+    def tastes(r):
+        for j in range(4):
+            mm(TASTE[j], C, uk(j)[0], uk(j)[1], v("qx%d" % r), v("sx%d" % r))
+
+    def base(r):
+        edges = [0] + [e for span in VSPANS[r] for e in span]
+        for i, (a, b) in enumerate(zip(edges, edges[1:])):
+            ts(v("base", 24 * r + a, 24 * r + b), v("num", 16 * a, 16 * b, 16), cq, op.subtract, 14.625 - 192 * (i % 2), op.add)
+
+    def run(plan, r, more):
+        steps = {"scores": lambda h: scores(r, h), "mask": mask, "keep": keep, "inner": inner, "sum": inner_sum,
+                 "compare": compare, "count": lambda k: count(r, k), "sums": lambda j: sums(r, j), "quad": quad,
+                 "pick": pick, "base": base, "signs": lambda j: signs(*SBLOCKS[r][j]), "tastes": lambda j: tastes(r),
+                 "places": lambda j: tt(v("ra", 0, 24), v("base", 24 * r, 24 * r + 24), v("dr", 15, C, 16), op.subtract)}
+        steps.update(more)
+        for step in plan.split():
+            name = step.rstrip("0123456789")
+            steps[name](int(step[len(name):]))
+
+    run(PLAN0, 0, {})
     for r in range(2):
         X, Y = xs[r], ys[r]
-        qx, sx = v("qx%d" % r), v("sx%d" % r)
-
-        def keep1(a, b):
-            tt(v("sm", a, b), sv(a, b), v("gate", a, b), op.min)
-
-        def keep2(a, b):
-            scan(v("sx", a, b), v("start", a, b), v("sm", a, b), -BIG, op.min, op.max)
-
-        keep1(192, LO)
-        keep1(0, 192)
-        keep1(LO, C)
-        keep2(192, LO)
-        keep2(0, 192)
-        keep2(LO, C)
-        for j in range(4):
-            mm(2 + j, C, uk(j)[0], uk(j)[1], qx, sx)
-
-        def compare(k):
-            for a, b in ((0, LO), (LO, 16 * k)):
-                ts(cmp_view(k, a, b), sv(a, b), col("sx", 16 * k + 15), op.is_lt)
-
-        def count(k):
-            e = 192 * (k - FIRSTV + 1)
-            scan(v("so", e - 8 * k, e), cmp_view(k, 0, 8 * k), cmp_view(k, 8 * k, 16 * k), -192.0, op.add, op.add)
-
-        def quad(i):
-            ks, n, c0 = QUADS[i]
-            quant(v("cc", c0, c0 + n), v("cs", c0, c0 + n), v("ct", 4 * c0, 4 * (c0 + n)))
-            mm(6, n, v("qb"), v("sb"), v("cc", c0, c0 + n), v("cs", c0, c0 + n), i == 0, i == len(QUADS) - 1)
-
-        def sign(k):
-            act(v("sg", 272 * k, 272 * k + 16 * k), v("ps0", 0, 16 * k), fn.Sign, bias=col("sx", 16 * k + 15), scale=-1.0)
-
-        turn = [15, 14, 13, 16] + list(range(12, 0, -1))
-        ahead = 0
-        for i, k in enumerate(turn):
-            while ahead < min(len(turn), i + (2 if k > 12 else 3 if k > 6 else 4)):
-                sign(turn[ahead])
-                ahead += 1
-            act(cmp_view(k, 0, 16 * k), v("sg", 272 * k, 272 * k + 16 * k), fn.Relu, acc=col("acc", k))
-        act(v("cq"), ps(3), fn.Copy)
-        act(v("cr"), ps(4), fn.Copy)
+        act(v("cq"), ps(TASTE[1]), fn.Copy)
+        act(v("cr"), ps(TASTE[2]), fn.Copy)
         if r == 0:
-            act(v("sel2"), v("t4"), fn.Sign, bias=cr, scale=-1.0)
-            act(v("val"), v("num", 0, C), fn.Identity, bias=ck, scale=4.0)
-            keeper("sel", "sel2", "osl", 4)
             later_constants()
-
-        tt(cmp_view(0, 0, LO), sv(0, LO), v("sx", 0, LO), op.is_le)
-        compare(23)
-        tt(cmp_view(0, LO, C), sv(LO, C), v("sx", LO, C), op.is_le)
-        compare(22)
-        count(23)
-        scan(v("dr"), v("keep16"), cmp_view(0, 0, C), 0.0, op.mult, op.add)
-        compare(21)
-        count(22)
-        if r == 0:
-            ts(v("base", 0, FIRSTV), v("num", 0, 16 * FIRSTV, 16), cq, op.subtract, 14.625, op.add)
-            ts(v("base", FIRSTV, 24), v("num", 16 * FIRSTV, C, 16), cq, op.subtract, 14.625 - 192, op.add)
-        compare(20)
-        count(21)
-        quad(0)
-        tt(v("ra", 0, 24), v("base"), v("dr", 15, C, 16), op.subtract)
-        compare(19)
-        count(20)
-        quad(2)
-        compare(18)
-        count(19)
-        compare(17)
-        count(18)
-        quad(3)
-        count(17)
-        quad(1)
-        quad(4)
-        cp(v("acc", FIRSTV, 24), v("so", 191, None, 192))
-        quad(5)
-        H = C // 2
 
         def test(out, bank, other, how, h):
             tt(v(out, H * h, H * h + H), v("ps%d" % bank, H * h, H * h + H), v(other, H * h, H * h + H), how)
 
+        def lower(h):
+            ts(v("y2", H * h, H * h + H), v("d2", H * h, H * h + H), col("col", 3), op.add, 0.0, op.is_gt)
+
+        fills = [lambda h=h, a=a: test(*a, h) for a in (("d1", TASTE[0], "cq", op.subtract), ("mrt", TASTE[3], "cr", op.max),
+                                                        ("d2", TASTE[0], "mrt", op.subtract)) for h in range(2)]
+        fills[2:2] = [lambda: act(v("y1"), v("d1"), fn.Sign, bias=col("col", 2))]
+        fills += [lambda: lower(0), lambda: lower(1)]
+
+        def filler(n=1):
+            for _ in range(min(n, len(fills))):
+                fills.pop(0)()
+
         tt(v("ra", 24, 48), v("ra", 0, 24), v("acc"), op.subtract)
         if r == 0:
-            quant(v("qe", 0, 256), v("se", 0, 256), v("et", 0, 1024))
+            pick(4)
         ts(v("ra", 48, 72), v("ra", 24, 48), 2.0 ** -13, op.mult)
-        test("d1", 2, "cq", op.subtract, 0)
-        scan(v("ex"), ps(6), v("sel16"), 0.0, op.add, op.mult)
-        test("d1", 2, "cq", op.subtract, 1)
+        scan(v("ex"), ps(SUMS), v("sel16"), 0.0, op.add, op.mult)
+        filler()
         tt(v("ra", 72, 96), v("ex", 15, C, 16), v("ra", 48, 72), op.add)
-        test("mrt", 5, "cr", op.max, 0)
+        filler()
         ts(v("rk"), v("ra", 72, 96), 8192.0, op.mult)
-        test("mrt", 5, "cr", op.max, 1)
-        act(v("y1"), v("d1"), fn.Sign, bias=col("col", 2))
-        o = ind(v("ord"), v("rk"))
-        issue("V", lambda o=o: g.vector.tensor_copy(o[0], T.val[:, :]), [v("ord")], [v("rk"), v("val")])
-        test("d2", 2, "mrt", op.subtract, 0)
+        filler(2)
+        scatter(v("ord"), v("rk"), v("val"))
+        filler()
         scan(v("osl"), v("ord", 0, 128), v("sel"), 0.0, op.add, op.mult)
-        test("d2", 2, "mrt", op.subtract, 1)
+        filler()
         ts(v("mo"), v("osl", 3, 128, 4), 8192.0, op.mult, -0.375, op.add)
-        ts(v("y2", 0, H), v("d2", 0, H), col("col", 3), op.add, 0.0, op.is_gt)
-        ts(v("y2", H, C), v("d2", H, C), col("col", 3), op.add, 0.0, op.is_gt)
+        filler()
         mt = "mt%d" % r
         act(v(mt, 256, 512), ind(v(X), v("mo", 16, 32)), fn.Copy)
         cp(v(mt, 0, 256), ind(v(X), v("mo", 0, 16)))
-        tt(v("ind", 0, 128), v("y1", 0, 128), v("y2", 0, 128), op.is_equal)
         qm, sm, lq, ls = v("qm%d" % r), v("sm%d" % r), v("lq%d" % r), v("ls%d" % r)
+        filler(2)
         quant(qm, sm, v(mt))
         wait("G", "V", total["V"])
         rid, pid = topo.addr(far[r])[:2]
         arr = "arr%d" % r
-        g.remote_dma(lq[0].bitcast(dt.uint8), qm[0].bitcast(dt.uint8), T.sem[arr], T.sem.sent, pid, rid, mask)
-        g.remote_dma(ls[0], sm[0], T.sem[arr], T.sem.sent, pid, rid, second[r])
+        g.remote_dma(lq[0].bitcast(dt.uint8), qm[0].bitcast(dt.uint8), T.sem[arr], T.sem.sent, pid, rid, topo.mask(core, far[r]))
+        g.remote_dma(ls[0], sm[0], T.sem[arr], T.sem.sent, pid, rid, topo.mask(core, far[r]))
 
-        tt(v("ind", 128, C), v("y1", 128, C), v("y2", 128, C), op.is_equal)
+        def standing(j):
+            tt(v("vk", A * j, A * j + A), v("cnt", A * j, A * j + A), v("ind", A * j, A * j + A), op.mult)
+
+        if r == 0:
+            pick_scales(4)
+            fills += weights()
+        tt(v("ind"), v("y1"), v("y2"), op.is_equal)
+        filler()
+        fill(v("alive", 0, A), 1.0)
         scan(v("cnt"), v("ind"), v("one", 0, C), col("col", 4), op.add, op.mult)
+        filler()
         ts(col("mu", 0), col("cnt", C - 1), col("col", 5), op.add)
-        tt(v("vk", 0, 128), v("cnt", 0, 128), v("ind", 0, 128), op.mult)
-        ts(v("mrow"), ind(v("num"), col("mu", 0)), 1.0 / LIFE, op.mult)
-        tt(v("vk", 128, C), v("cnt", 128, C), v("ind", 128, C), op.mult)
-        for k in range(4):
-            act(v("tab", 256 * k + 112, 256 * k + 128), v("m16", 0, 16), fn.Identity, scale=col("mrow", k))
-        wait("Y", "sent", 2 * (r + 1) * engines)
-        for h in range(2):
-            for k in range(4):
-                dma("Y", "tr%d" % r, v("tin", 32 * k + 16 * h, 32 * k + 16 * h + 16),
-                    v("vk", rows=slice(16 * h + k, 128, 32)))
+        filler()
+        standing(0)
+        tt(v("mrow", 16, 32), ind(v("num"), col("mu", 0)), v("wa"), op.mult)
+        filler()
+        standing(1)
+        tt(v("mrow", 0, 16), v("mrow", 16, 32), v("wb"), op.add)
 
-        wait("P", arr, 2 * engines)
+        def turn_standings():
+            standing(2)
+            wait("Y", "sent", sent[r])
+            for h in range(2):
+                for k in range(4):
+                    dma("Y", "tr%d" % r, v("tin", 32 * k + 16 * h, 32 * k + 16 * h + 16),
+                        v("vk", rows=slice(16 * h + k, 128, 32)))
+
+        wait("P", arr, 2 * len(topo.engines(far[r], core)))
         mm(1, A, uk(4)[0], uk(4)[1], lq, ls)
         mm(0, A, uk(4)[0], uk(4)[1], lq, ls)
 
-        def objects():
+        def objects(b):
+            qe, se = v("qe", 128 * b, 128 * b + 128), v("se", 128 * b, 128 * b + 128)
             if r == 0:
-                quant(v("qe", 256, 512), v("se", 256, 512), v("et", 1024, 2048))
-            for b in range(4):
-                mm(2 + b, A, v("qe", 128 * b, 128 * b + 128), v("se", 128 * b, 128 * b + 128), lq, ls)
+                quant(qe, se, v("et", 512 * b, 512 * b + 512))
+            mm(2 + b, A, qe, se, lq, ls)
 
-        spare_s = {t: [] for t in range(TICKS)}
-        spare_s[0].append(lambda: act(v("win", 0, 512, 4), ps(0, A), fn.Copy))
-        for b in range(4):
-            spare_s[b + 1].append(lambda b=b: act(v("bh", b, 512, 4), ps(2 + b, A), fn.Identity, scale=0.5))
-            if r == 0:
-                spare_s[b].append(lambda b=b: act(v("ya", C * b, C * b + C), v(X, b, 4 * C, 4), fn.Identity, scale=32.0))
-            spare_s[b + 4].append(lambda b=b: act(v("xh", C * b, C * b + C), v(Y, C * b, C * b + C), fn.Identity, scale=1.0 / 64))
-        spare_s[8].append(lambda: act(v("bm", 0, 128), ind(v("bh"), v("ho", 0, 8)), fn.Copy))
-        spare_v = {
-            0: [objects],
-            1: [lambda: quant(v("qv"), v("sv"), v("vt"))] if r == 0 else [],
-            2: [],
-            3: [lambda: issue("V", lambda: g.vector.transpose(T.tout[:, :], T.tin[:, :]), [v("tout")], [v("tin")])],
-            4: [lambda: tt(v("s64"), v("tout", 0, 64), v("tout", 64, 128), op.add)],
-            5: [lambda: tt(v("s32"), v("s64", 0, 32), v("s64", 32, 64), op.add)],
-            6: [lambda: ts(v("fi"), v("s32"), 0.1, op.mult, -0.46, op.add)],
-            7: [lambda: ts(v("f10"), v("fi"), -10.0, op.mult)],
-            8: [lambda: tt(v("slot"), v("s32"), v("f10"), op.add),
-                lambda: ts(v("ho", 0, 8), v("ee", 0, 8), 4.0, op.mult, cr, op.add)],
-            9: [lambda b=b: ts(v("zo", 24 * b, 24 * b + 24), v("slot", 0, 24), 16.0, op.mult, 4.0 * b, op.add) for b in range(4)],
+        def slots(b):
+            ts(v("zo", 24 * b, 24 * b + 24), v("slot", 0, 24), 16.0, op.mult, 4.0 * b, op.add)
+
+        spare = {
+            1: [lambda b=b: objects(b) for b in range(3)],
+            2: [lambda: objects(3)] + [lambda: quant(v("qv"), v("sv"), v("vt")), lambda: base(1)][2 * r:],
+            4: [lambda: issue("V", lambda: g.vector.transpose(T.tout[:, :], T.tin[:, :]), [v("tout")], [v("tin")]),
+                lambda: tt(v("s64"), v("tout", 0, 64), v("tout", 64, 128), op.add),
+                lambda: tt(v("s32"), v("s64", 0, 32), v("s64", 32, 64), op.add)],
+            5: [lambda: ts(v("fi"), v("s32"), 0.1, op.mult, -0.46, op.add),
+                lambda: ts(v("f10"), v("fi"), -10.0, op.mult),
+                lambda: tt(v("slot"), v("s32"), v("f10"), op.add)],
+            6: [lambda b=b: slots(b) for b in range(3)],
+            7: [lambda: slots(3)],
+            8: [lambda: ts(v("ho", 0, 8), v("ee", 0, 8), 4.0, op.mult, cr, op.add)],
         }
         for t in range(TICKS):
+            fills = list(spare.get(t, []))
+            scan(v("rm"), ps(1, A) if t == 0 else v("msk", 0, A), v("low"), -BIG, op.max, op.max)
+            act(v("step", 1, A + 1), v("rm"), fn.Sign, bias=col("rm", A - 1), scale=-1.0, acc=col("ee", t))
             if t == 0:
-                scan(v("rm"), ps(1, A), v("low"), -BIG, op.max, op.max)
-            else:
-                cp(v("msk"), ind(v("win"), v("o1", 8 * t, 8 * t + 8)))
-                scan(v("rm"), v("msk"), v("low"), -BIG, op.max, op.max)
-            act(v("junk", A * t, A * t + A), v("rm"), fn.Sign, bias=col("rm", A - 1), scale=-1.0, acc=col("ee", t))
-            for f in spare_v[t] + spare_s[t]:
-                f()
-            if t + 1 < TICKS:
-                ts(v("o5", 2 * t, 2 * t + 2), v("c5"), col("ee", t), op.add)
-                tt(v("cw", 32 * t + 32, 32 * t + 64), ind(v("tab"), v("o5", 2 * t, 2 * t + 2)), v("cw", 32 * t, 32 * t + 32), op.add)
-                scan(v("sc"), v("keep4"), v("cw", 32 * t + 32, 32 * t + 64), 0.0, op.mult, op.add)
-                cp(v("o1", 8 * t + 8, 8 * t + 16), v("sc", 3, 32, 4))
+                act(v("msk", 0, A), ps(0, A), fn.Copy)
+                turn_standings()
+            if t < 4:
+                act(v("xh", C * t, C * t + C), v(X, t, 4 * C, 4), fn.Identity, scale=0.5)
+            elif t < 8:
+                act(v("bh", t - 4, 512, 4), ps(t - 2, A), fn.Identity, scale=0.5)
+                if r == 0:
+                    act(v("ya", C * (t - 4), C * (t - 3)), v(X, t - 4, 4 * C, 4), fn.Identity, scale=32.0)
+            if t + 1 == TICKS:
+                break
+            now = v("mrow", 0, 16) if t == 0 else v("ww", 16 * t, 16 * t + 16)
+            if t > 0:
+                old = v("mrow", 0, 16) if t == 1 else v("ww", 16 * t - 16, 16 * t)
+                tt(v("wt", 16, 32), ind(v("alive"), col("o5", 4 * t - 2)), old, op.mult)
+                tt(now, v("wt", 16, 32), v("mrow", 0, 16), op.add)
+            ts(v("o5", 4 * t, 4 * t + 3), v("c5", 0, 3), col("ee", t), op.add, A + 1.0, op.min)
+            tt(v("wt", 32, 48), ind(v("step"), col("o5", 4 * t)), now, op.mult)
+            filler()
+            minus_sum(col("sc", t), v("wt", 32, 48))
+            filler()
+            ts(col("o1", 2 * t), col("sc", t), col("ee", t), op.max, col("col", 7), op.min)
+            filler()
+            scatter(v("msk"), col("o1", 2 * t), v("low", 0, 16))
+            if t + 2 < TICKS:
+                scatter(v("alive"), col("o1", 2 * t), v("vk", C, C + 16))
+            if t == 8:
+                act(v("bm", 0, 128), ind(v("bh"), v("ho", 0, 8)), fn.Copy)
 
         ts(v("ho", 8, TICKS), v("ee", 8, TICKS), 4.0, op.mult, cr, op.add)
         if r == 1:
             cp(v("ho2"), v("ee", 0, TICKS))
         cp(v("bm", 128, 160), ind(v("bh"), v("ho", 8, TICKS)))
-        if r == 1:
-            act(v("erow"), ind(v("num"), v("ho2")), fn.Copy)
-            act(v("lrow"), ind(v("erow"), v("zo", 0, 24)), fn.Copy)
-            dma("Y", "out", (T.ol[:, :], []), v("lrow", rows=slice(0, 128, 16)))
         zt = "zt%d" % r
-        banks = ((2, 3, 4, 5), (6, 7, 0, 1))
         Xn, Yn, qn, sn = xs[r + 1], ys[r + 1], "qx%d" % (r + 1), "sx%d" % (r + 1)
 
-        def take(h, b):
-            a, e = cols[h]
-            tt(v(zt, 4 * a + b, 4 * e, 4), ind(v("bm"), v("zo", 24 * b + a // 16, 24 * b + e // 16)),
-               v("xh", C * b + a, C * b + e), op.add)
+        def planar(name, j):
+            (a, e), b = CUTS[j // 4], j % 4
+            return v(name, C * b + a, C * b + e)
+
+        def tiled(name, j):
+            (a, e), b = CUTS[j // 4], j % 4
+            return v(name, 4 * a + b, 4 * e, 4)
+
+        def chosen(j):
+            (a, e), b = CUTS[j // 4], j % 4
+            return ind(v("bm"), v("zo", 24 * b + a // 16, 24 * b + e // 16))
+
+        for j in FETCH:
+            act(planar("got", j), chosen(j), fn.Copy)
+
+        def take(j):
+            tt(tiled(zt, j), planar("got", j) if j in FETCH else chosen(j), planar("xh", j), op.add)
 
         def layer(h):
-            a, e = cols[h]
+            a, e = CUTS[h]
             qz, sz = v("qz%d" % r, a, e), v("sz%d" % r, a, e)
             quant(qz, sz, v(zt, 4 * a, 4 * e))
             for b in range(4):
-                mm(banks[h][b], e - a, v("qw", 128 * b, 128 * b + 128), v("sw", 128 * b, 128 * b + 128), qz, sz)
+                mm(LAYER[h][b], e - a, v("qw", 128 * b, 128 * b + 128), v("sw", 128 * b, 128 * b + 128), qz, sz)
 
-        def renew(h, b):
-            a, e = cols[h]
-            yn = v(Yn, C * b + a, C * b + e)
-            tt(yn, ps(banks[h][b], e - a), v(Y, C * b + a, C * b + e), op.add)
-            if b < 3 - h:
-                act(v(Xn, 4 * a + b, 4 * e, 4), yn, fn.Identity, scale=1.0 / 32)
+        def renew(j):
+            tt(planar(Yn, j), ps(LAYER[j // 4][j % 4], A), planar(Y, j), op.add)
+            if j not in OWN[r]:
+                act(tiled(Xn, j), planar(Yn, j), fn.Identity, scale=1.0 / 32)
 
-        def shrink(h, b):
-            a, e = cols[h]
-            ts(v(Xn, 4 * a + b, 4 * e, 4), v(Yn, C * b + a, C * b + e), 1.0 / 32, op.mult)
+        def shrink(j):
+            ts(tiled(Xn, j), planar(Yn, j), 1.0 / 32, op.mult)
 
-        for b in range(4):
-            take(0, b)
-        take(1, 0)
-        layer(0)
-        for b in range(1, 4):
-            take(1, b)
-        renew(0, 0)
-        layer(1)
-        for b in range(1, 4):
-            renew(0, b)
-        renew(1, 0)
-        renew(1, 1)
-        shrink(0, 3)
-        renew(1, 2)
-        renew(1, 3)
-        for h in range(2):
-            a, e = cols[h]
-            scores(r + 1, h)
-            if h == 0:
-                shrink(1, 2)
-                shrink(1, 3)
-            if r + 1 == len(STEPS):
-                mm(2 + h, e - a, v("qv"), v("sv"), v(qn, a, e), v(sn, a, e))
-                dma("Y", "out", (T.oc[:, 4 * a:4 * e], []), bytes_of(v(qn, a, e)))
-                act(v("yo", a, e), ps(2 + h, e - a), fn.Copy)
-                dma("S", "out", (T.y[:, a:e], []), v("yo", a, e))
+        def lists(j):
+            if j == 0:
+                act(v("erow"), ind(v("num"), v("ho2")), fn.Copy)
+            else:
+                act(v("lrow"), ind(v("erow"), v("zo", 0, 24)), fn.Copy)
+
+        def codes(h):
+            a, e = CUTS[h]
+            quant(v(qn, a, e), v(sn, a, e), v(Xn, 4 * a, 4 * e))
+            mm(LAST[h], e - a, v("qv"), v("sv"), v(qn, a, e), v(sn, a, e))
+            dma("Y", "out", (T.oc[:, 4 * a:4 * e], []), bytes_of(v(qn, a, e)))
+
+        def store(h):
+            a, e = CUTS[h]
+            act(v("yo", a, e), ps(LAST[h], e - a), fn.Copy)
+            dma("S", "out", (T.y[:, a:e], []), v("yo", a, e))
+
+        run(PLAN1 if r + 1 < len(STEPS) else PLAN2, r + 1,
+            {"take": take, "layer": layer, "renew": renew, "shrink": shrink, "lists": lists, "codes": codes, "store": store})
     for k in range(4):
         dma("Y", "out", (T.osc[4 * k:4 * k + 4, :], []), v("sx2", rows=slice(32 * k, 32 * k + 4)))
-    g.wait_ge(T.sem.sent, 2 * len(STEPS) * engines)
+    dma("Y", "out", (T.ol[:, :], []), v("lrow", rows=slice(0, 128, 16)))
+    g.wait_ge(T.sem.sent, sent[-1])
     for sem in sorted(total):
         wait("G", sem, total[sem])

from concourse.mybir import dt, AluOpType, ActivationFunctionType, AxisListType

C, A, LIFE, TICKS = 384, 128, 128, 10
STEPS = [1, 2]
BIG = 1e29
EPS = 2.0 ** -100
UNIT = 512.0
F32, BF, I32, U16, X4, U8 = "float32", "bfloat16", "int32", "uint16", "float8_e4m3fn_x4", "uint8"
QUADS = [([0, 21, 22, 23], 384, 0), ([17, 18, 19, 20], 320, 384), ([13, 14, 15, 16], 256, 704),
         ([9, 10, 11, 12], 192, 960), ([5, 6, 7, 8], 128, 1152), ([1, 2, 3, 4], 128, 1280)]
QCOLS = 1408
CUTS = [(0, 128), (128, 256), (256, C)]
VSPANS = [[(14, 16), (19, 24)], [(13, 16), (20, 24)]]
SBLOCKS = [[(0, [7, 6, 5]), (1, [13, 12, 11, 10]), (2, [16, 17, 18]), (1, [9, 8, 4, 3, 2, 1])],
           [(0, [7, 6, 5]), (1, [12, 11, 10, 9]), (2, [16, 17, 18, 19]), (1, [8, 4, 3, 2, 1])]]
SG = 16 * 21
FETCH = (2, 3, 6, 7, 9, 10, 11)
OWN = [(3, 7, 8, 9, 10, 11), (3, 7, 11)]
PLAN0 = ("pick0 scores0 base0 pick1 scores1 mask0 pick2 keep0 signs0 scores2 mask1 inner0 keep1 signs1 pick3 "
         "compare15 mask2 compare14 inner1 keep2 signs2 signs3 count14 sum0 count15 sum1 "
         "compare23 compare22 inner2 tastes0 compare21 sum2 compare20 count23 quad0 compare19 count22 "
         "quad2 count21 quad1 count20 quad3 count19 quad4 places0 sums0 sums1 quad5")
TAKE = ("take0 take1 take4 take2 take3 take5 layer0 take6 take7 take8 layer1 %s renew0 renew1 take9 renew2 renew3 "
        "take10 take11 shrink3 renew4 ")
PLAN1 = TAKE % "" + (
    "scores0 renew5 layer2 renew6 renew7 mask0 shrink7 keep0 signs0 scores1 renew8 inner0 renew9 renew10 renew11 "
    "shrink8 mask1 shrink9 shrink10 shrink11 keep1 signs1 scores2 inner1 compare15 compare13 sum1 mask2 compare14 sum0 "
    "keep2 signs2 signs3 tastes0 count15 count14 count13 compare23 compare22 inner2 compare21 sum2 compare20 quad0 "
    "count23 quad2 count22 quad3 count21 quad1 count20 quad4 places0 sums0 sums1 quad5")
PLAN2 = TAKE % "lists0" + (
    "codes0 renew5 layer2 renew6 renew7 store0 shrink7 renew8 codes1 renew9 renew10 renew11 store1 shrink11 codes2 "
    "lists1 store2")
PARTS = {"s64": ("small", 0, 64), "s32": ("small", 64, 32), "f10": ("small", 96, 32), "slot": ("small", 128, 32),
         "ho": ("hist", 0, TICKS), "ho2": ("hist", TICKS, TICKS),
         "sgr": ("wts", 0, 16), "wa": ("wts", 16, 16), "wb": ("wts", 32, 16)}


def _sb(n, d):
    return ("sbuf", [128, n], d)


SCRATCH = {
    "x0": _sb(4 * C, BF), "x1": _sb(4 * C, BF), "x2": _sb(4 * C, BF),
    "ut": _sb(512, BF), "vt": _sb(512, BF),
    "qu": _sb(128, X4), "su": _sb(128, U8), "qv": _sb(128, X4), "sv": _sb(128, U8),
    "qa": _sb(128, X4), "sa": _sb(128, U8), "qk": _sb(640, X4), "sk": _sb(640, U8),
    "qw": _sb(512, X4), "sw": _sb(512, U8),
    "one": _sb(512, BF), "et": _sb(2048, BF), "qe": _sb(512, X4), "se": _sb(512, U8),
    "bt": _sb(512, BF), "qb": _sb(128, X4), "sb": _sb(128, U8),
    "pi": _sb(16, I32), "pf": _sb(16, F32), "col": _sb(16, F32),
    "g16": _sb(8, F32), "t16": _sb(C, BF), "t4": _sb(128, F32), "num": _sb(400, F32),
    "uaf": _sb(8, U16), "g40": _sb(40, F32), "uko": _sb(40, U16),
    "gate": _sb(C, BF), "start": _sb(C, F32), "keep16": _sb(C, BF),
    "sel16": _sb(C, BF), "base": _sb(48, F32),
    "val": _sb(C, F32), "sel": _sb(128, F32), "sel2": _sb(128, F32),
    "c5": _sb(4, F32), "low": _sb(128, F32), "wts": _sb(48, F32),
    "sm": _sb(C, F32), "sx": _sb(C, F32), "dr": _sb(C, BF), "ct": _sb(4 * QCOLS, BF), "cc": _sb(QCOLS, X4),
    "cs": _sb(QCOLS, U8), "so": _sb(7 * 192, BF), "sg": _sb(SG * SG // 16, BF),
    "acc": _sb(24, F32), "ra": _sb(96, F32), "ex": _sb(C, F32), "rk": _sb(24, U16),
    "ord": _sb(C, F32), "osl": _sb(128, F32), "mo": _sb(32, U16),
    "cq": _sb(C, F32), "cr": _sb(C, F32), "mrt": _sb(C, F32), "d1": _sb(C, BF), "d2": _sb(C, BF),
    "y1": _sb(C, BF), "y2": _sb(C, BF), "ind": _sb(C, BF), "cnt": _sb(C, F32), "vk": _sb(512, F32),
    "mu": _sb(2, U16), "mrow": _sb(32, F32),
    "tin": _sb(128, F32), "tout": _sb(128, F32), "small": _sb(160, F32), "fi": _sb(32, I32), "zo": _sb(96, U16),
    "msk": _sb(144, F32), "alive": _sb(144, F32), "rm": _sb(128, F32), "step": _sb(144, F32), "ee": _sb(16, F32),
    "o5": _sb(4 * TICKS, U16), "ww": _sb(16 * TICKS, F32), "wt": _sb(48, F32), "sc": _sb(TICKS, F32),
    "o1": _sb(2 * TICKS, U16),
    "bh": _sb(512, F32), "hist": _sb(2 * TICKS, U16), "bm": _sb(160, F32), "erow": _sb(160, F32),
    "lrow": _sb(C, F32),
    "xh": _sb(4 * C, BF), "got": _sb(4 * C, BF), "ya": _sb(4 * C, BF), "yb": _sb(4 * C, BF), "yc": _sb(4 * C, BF),
    "yo": _sb(C, F32), "qx2": _sb(C, X4), "sx2": _sb(C, U8),
}
for _r in range(2):
    SCRATCH.update({"qx%d" % _r: _sb(C, X4), "sx%d" % _r: _sb(C, U8), "mt%d" % _r: _sb(512, BF),
                    "qm%d" % _r: _sb(A, X4), "sm%d" % _r: _sb(A, U8), "lq%d" % _r: _sb(A, X4), "ls%d" % _r: _sb(A, U8),
                    "zt%d" % _r: _sb(4 * C, BF), "qz%d" % _r: _sb(C, X4), "sz%d" % _r: _sb(C, U8)})
for _b in range(8):
    SCRATCH["ps%d" % _b] = ("psum", [128, 512], F32)

SEMAPHORES = ["V", "S", "P", "G", "lx0", "lx1", "lx2", "lu", "lv", "lwc", "lws", "tr0", "tr1", "out", "sent", "arr0", "arr1"]


def rank_program(g, core, T, topo):
    rank = T.rank_of(core)
    if rank is None:
        return
    op, fn = AluOpType, ActivationFunctionType
    queue = {"V": g.vector, "S": g.scalar, "P": g.tensor, "G": g, "Y": g.sync}
    total = {}
    known = {q: {} for q in queue}
    clock = {}
    touched = {}
    group = {}

    def v(name, a=0, b=None, s=1, rows=None):
        if name in PARTS:
            name, first, n = PARTS[name]
            a, b = a + first, first + (n if b is None else b)
        if b is None:
            b = T[name].shape[1]
        m = 0
        if s == 1:
            m = (1 << b) - (1 << a)
        else:
            for i in range(a, b, s):
                m |= 1 << i
        r = slice(None) if rows is None else rows
        return (T[name][r, a:b] if s == 1 else T[name][r, a:b:s], [(name, m)])

    def ind(w, o, cast=None):
        ap = w[0] if cast is None else w[0].bitcast(cast)
        return (ap.indirect(o[0]), w[1] + o[1])

    def wait(q, sem, n):
        if known[q].get(sem, 0) >= n:
            return
        queue[q].wait_ge(T.sem[sem], n)
        known[q][sem] = n
        for s2, n2 in clock.get((sem, n), {}).items():
            if known[q].get(s2, 0) < n2:
                known[q][s2] = n2

    def issue(q, call, writes, reads, sem=None, inc=1, adds=False):
        sem = sem or q
        need = {}
        uses = [(b, m, True) for w in writes for b, m in w[1]]
        uses += [(b, m, False) for r in reads if isinstance(r, tuple) for b, m in r[1]]
        for b, m, wr in uses:
            bank = b.startswith("ps")
            if bank and adds:
                continue
            for s2, n2, m2, w2, q2 in touched.get(b, []):
                if (bank and (q2 != q or wr or w2)) or (m & m2 and (wr or w2)):
                    n2 = group.get(s2, n2)
                    if s2 != sem or s2 not in group:
                        need[s2] = max(need.get(s2, 0), n2)
        for s2 in sorted(need, key=lambda z: z == q):
            wait(q, s2, need[s2])
        total[sem] = total.get(sem, 0) + inc
        call().then_inc(T.sem[sem], inc)
        n = total[sem]
        key = (sem, group.get(sem, n))
        old = clock.get(key, {})
        clock[key] = {z: max(old.get(z, 0), known[q].get(z, 0)) for z in set(old) | set(known[q])}
        for b, m, wr in uses:
            lst = touched.setdefault(b, [])
            if wr:
                lst[:] = [e for e in lst if e[2] & ~m and not b.startswith("ps")]
            lst.append((sem, n, m, wr, q))

    def ap(x):
        return x[0] if isinstance(x, tuple) else x

    def ts(o, i, s1, o0, s2=None, o1=None):
        if o1 is None:
            issue("V", lambda: g.vector.tensor_scalar(o[0], i[0], ap(s1), None, o0), [o], [i, s1])
        else:
            issue("V", lambda: g.vector.tensor_scalar(o[0], i[0], ap(s1), ap(s2), o0, o1), [o], [i, s1, s2])

    def tt(o, a, b, o0):
        issue("V", lambda: g.vector.tensor_tensor(o[0], a[0], b[0], o0), [o], [a, b])

    def cp(o, i):
        issue("V", lambda: g.vector.tensor_copy(o[0], i[0]), [o], [i])

    def scatter(window, offsets, i):
        issue("V", lambda: g.vector.tensor_copy(window[0].indirect(offsets[0]), i[0]), [window], [offsets, i])

    def scan(o, a, b, init, o0, o1):
        issue("V", lambda: g.vector.tensor_tensor_scan(o[0], a[0], b[0], ap(init), o0, o1), [o], [a, b, init])

    def minus_sum(o, i):
        issue("V", lambda: g.vector.tensor_reduce(o[0], i[0], AxisListType.X, op.add, negate=True), [o], [i])

    def fill(o, c):
        issue("V", lambda: g.vector.memset(o[0], c), [o], [])

    def quant(q, s, i):
        issue("V", lambda: g.vector.quantize_mx(q[0], s[0], i[0]), [q, s], [i])

    def act(o, i, f, bias=0.0, scale=1.0, acc=None):
        if f == fn.Copy:
            issue("S", lambda: g.scalar.activation(o[0], i[0], f), [o], [i])
        elif acc is None:
            issue("S", lambda: g.scalar.activation(o[0], i[0], f, bias=ap(bias), scale=ap(scale)), [o], [i, bias, scale])
        else:
            issue("S", lambda: g.scalar.activation(o[0], i[0], f, bias=ap(bias), scale=ap(scale), accum_out=acc[0]),
                  [o, acc], [i, bias, scale])

    def mm(bank, n, wq, ws, xq, xs, start=True, stop=True):
        o = v("ps%d" % bank, 0, n)
        issue("P", lambda: g.tensor.matmul_mx(o[0], wq[0], ws[0], xq[0], xs[0], start, stop), [o], [wq, ws, xq, xs],
              adds=not start)

    def iota(o, pattern, base=0, cm=0, small=True):
        if small:
            issue("G", lambda: g.iota(o[0], pattern, base, cm, allow_small_or_imprecise_dtypes=True), [o], [])
        else:
            issue("G", lambda: g.iota(o[0], pattern, base, cm), [o], [])

    def dma(q, sem, o, i):
        issue(q, lambda: queue[q].dma_start(o[0], i[0]), [o], [i], sem=sem, inc=16)

    def ps(b, n=C):
        return v("ps%d" % b, 0, n)

    def col(name, j):
        return v(name, j, j + 1)

    def bytes_of(x):
        return (x[0].bitcast(dt.uint8), x[1])

    def words_of(x):
        return (x[0].bitcast(dt.uint32), x[1])

    group["tr0"] = group["tr1"] = 8 * 16
    group["out"] = 11 * 16
    H = C // 2

    dma("S", "lu", v("ut"), (T.u[:, :], []))
    for h, (a, b) in enumerate(CUTS):
        dma("Y", "lx%d" % h, v("x0", 4 * a, 4 * b), (T.x[:, 4 * a:4 * b], []))
    wait("Y", "lx2", 16)
    dma("Y", "lwc", bytes_of(v("qw")), (T.wc[:, :], []))
    dma("Y", "lws", v("sw"), (T.ws[:, :], []))
    dma("Y", "lv", v("vt"), (T.v[:, :], []))

    iota(v("g16"), [[16, 8]])
    iota(col("pi", 0), [[0, 1]], 0, 1, small=False)
    iota(v("t16"), [[0, 24], [1, 16]])
    iota(v("g40"), [[1, 5], [16, 8]], 4)
    iota(v("num"), [[1, 400]])
    iota(v("t4"), [[0, 32], [1, 4]])

    def blank(quads):
        for ks, n, c0 in quads:
            fill(v("ct", 4 * (c0 + 16 * min(k for k in ks if k)), 4 * (c0 + n)), 0.0)

    fill(v("one"), 1.0)
    blank(QUADS[:2])
    cp(v("uaf"), v("g16"))
    ts(col("pi", 1), col("pi", 0), 15, op.bitwise_and)
    ts(col("pi", 2), col("pi", 0), 3, op.bitwise_and)
    ts(col("pi", 3), col("pi", 0), 2, op.logical_shift_right, 3, op.bitwise_and)
    ts(col("pi", 4), col("pi", 0), 1, op.bitwise_and)
    ts(col("pi", 5), col("pi", 0), 2, op.bitwise_and)
    ts(col("pi", 6), col("pi", 0), 112, op.bitwise_and)
    blank(QUADS[2:5])
    cp(v("pf", 0, 7), v("pi", 0, 7))
    blank(QUADS[5:])
    cq, ck, cr, b1, b2 = col("pf", 1), col("pf", 2), col("pf", 3), col("pf", 4), col("pf", 5)
    ts(v("pf", 8, 16), v("g16"), col("pf", 6), op.is_equal)
    ts(v("gate"), v("t16"), cq, op.not_equal, -2 * BIG, op.mult)
    for j in range(8):
        act(v("bt", 64 * j, 64 * j + 64), v("one", 0, 64), fn.Identity, scale=col("pf", 8 + j))
    for b in range(4):
        issue("G", lambda b=b: g.affine_select(T.et[:, 512 * b:512 * b + 512], T.one[:, :], [[-1, 512]], op.is_equal, 0.0, b, 4),
              [v("et", 512 * b, 512 * b + 512)], [v("one")])
    for name, n in (("msk", 144), ("low", 128)):
        issue("G", lambda name=name, n=n: g.affine_select(T[name][:, :], T.one[:, 0:n], [[0, n]], op.is_equal, -BIG, 1, 0),
              [v(name)], [v("one")])
    iota(v("step"), [[0, 144]], 1)
    iota(v("alive", A, 144), [[0, 16]])
    iota(v("vk", C, 512), [[0, 128]])
    act(col("acc", 0), ck, fn.Identity, scale=0.0)
    act(v("start"), v("t16"), fn.Identity, bias=-BIG, scale=2 * BIG)
    act(v("keep16"), v("t16"), fn.Sign)

    def later_constants():
        act(v("sel2"), v("t4"), fn.Sign, bias=cr, scale=-1.0)
        act(v("val"), v("num", 0, C), fn.Identity, bias=ck, scale=4.0)
        act(v("osl"), v("sel2"), fn.Abs, bias=-0.5, scale=-8192.0)
        act(col("col", 2), b1, fn.Identity, bias=EPS, scale=-2.0 * EPS)
        act(col("col", 3), b2, fn.Identity, bias=EPS, scale=-EPS)
        act(col("col", 7), cq, fn.Identity, bias=float(A))
        act(col("col", 6), cr, fn.Relu, bias=-1000.0, scale=1000.0)
        act(v("sel"), v("osl"), fn.Relu, bias=8192.5, scale=-1.0)
        act(col("col", 4), ck, fn.Identity, bias=-1.0, scale=1.0 / 16)
        act(col("col", 5), ck, fn.Identity, bias=1.0, scale=-1.0 / 16)
        act(v("c5", 0, 2), v("one", 0, 2), fn.Identity, bias=col("col", 6), scale=cr)
        act(v("c5", 2, 4), v("one", 0, 2), fn.Identity, bias=col("col", 6), scale=0.0)
        act(v("sel", 3, None, 4), v("sel2", 3, None, 4), fn.Identity, bias=2.0 ** -13, scale=2.0 ** -13 - 2.0 ** -26)

    def weights():
        fill(v("sgr", 0, 4), UNIT)
        fill(v("sgr", 4, 8), -UNIT)
        fill(v("sgr", 8, 16), 0.0)
        ts(v("wt", 0, 16), v("t4", 0, 16), ck, op.is_ge)
        return [lambda: tt(v("wa"), v("wt", 0, 16), v("sgr"), op.mult),
                lambda: tt(v("wt", 16, 32), v("wa"), v("sgr"), op.subtract),
                lambda: ts(v("wb"), v("wt", 16, 32), 4096.0, op.mult),
                lambda: ts(col("wb", 8), cr, -2.0 ** 30, op.mult, (0.5 - LIFE) * UNIT, op.add)]

    ts(v("d1"), v("t16"), cq, op.is_equal, 8192.0, op.mult)
    ts(v("d2"), v("t16"), cq, op.is_gt)
    ts(v("uko", 0, 8), v("g40", 0, 8), ck, op.add)
    ts(v("uko", 8, 16), v("g40", 8, 16), b2, op.add, b1, op.subtract)
    ts(v("uko", 16, 24), v("g40", 16, 24), b1, op.add, b2, op.subtract)
    ts(v("uko", 24, 32), v("g40", 24, 32), ck, op.subtract)
    tt(v("sel16"), v("d1"), v("d2"), op.add)
    ts(v("uko", 32, 40), v("g40", 32, 40), ck, op.add)
    quant(v("qu"), v("su"), v("ut"))
    quant(v("qb"), v("sb"), v("bt"))
    ts(v("sel16", 15, C, 16), v("sel16", 15, C, 16), 2.0 ** -26, op.mult)
    cp(words_of(v("qa")), ind(v("qu"), v("uaf"), dt.uint32))
    act(v("sa"), ind(v("su"), v("uaf")), fn.Copy)

    def pick(j):
        cp(words_of(v("qk", 128 * j, 128 * j + 128)), ind(v("qu"), v("uko", 8 * j, 8 * j + 8), dt.uint32))

    def pick_scales(j):
        act(v("sk", 128 * j, 128 * j + 128), ind(v("su"), v("uko", 8 * j, 8 * j + 8)), fn.Copy)

    for j in range(4):
        pick_scales(j)

    far = [T.cores[rank ^ s] for s in STEPS]
    sent = [2 * sum(len(topo.engines(core, p)) for p in far[:r + 1]) for r in range(len(far))]

    def uk(j):
        return v("qk", 128 * j, 128 * j + 128), v("sk", 128 * j, 128 * j + 128)

    place = {k: (c0, s) for ks, n, c0 in QUADS for s, k in enumerate(ks)}

    def cmp_view(k, a, b):
        c0, s = place[k]
        return v("ct", 4 * (c0 + a) + s, 4 * (c0 + b), 4)

    xs, ys = ["x0", "x1", "x2"], ["ya", "yb", "yc"]
    VS, SS, SUMS, TASTE = (4, 2, 6), (5, 3, 7), 0, (1, 4, 5, 2)
    LAYER, LAST = ((4, 5, 6, 7), (0, 1, 2, 3), (6, 7, 0, 1)), (4, 5, 2)

    def part(h):
        return v("ps%d" % VS[h], *CUTS[h])

    def scores(r, h):
        a, b = CUTS[h]
        quant(v("qx%d" % r, a, b), v("sx%d" % r, a, b), v(xs[r], 4 * a, 4 * b))
        if h == 2:
            mm(SUMS, b - a, v("qa"), v("sa"), v("qx%d" % r, a, b), v("sx%d" % r, a, b))
        for bank in (VS[h], SS[h]):
            mm(bank, b, v("qa"), v("sa"), v("qx%d" % r, 0, b), v("sx%d" % r, 0, b))

    def mask(h):
        tt(v("sm", *CUTS[h]), ps(SUMS, A) if h == 2 else part(h), v("gate", *CUTS[h]), op.add)

    def keep(h):
        scan(v("sx", *CUTS[h]), v("start", *CUTS[h]), v("sm", *CUTS[h]), -BIG, op.min, op.max)

    def inner(h):
        tt(cmp_view(0, *CUTS[h]), part(h), v("sx", *CUTS[h]), op.is_le)

    def inner_sum(h):
        scan(v("dr", *CUTS[h]), v("keep16", *CUTS[h]), cmp_view(0, *CUTS[h]), 0.0, op.mult, op.add)

    def compare(k):
        ts(cmp_view(k, 0, 16 * k), ps(VS[k // 8], 16 * k), col("sx", 16 * k + 15), op.is_lt)

    def end(r, k):
        return 192 * (1 + [j for a, b in VSPANS[r] for j in range(a, b)].index(k))

    def count(r, k):
        e = end(r, k)
        scan(v("so", e - 8 * k, e), cmp_view(k, 0, 8 * k), cmp_view(k, 8 * k, 16 * k), -192.0, op.add, op.add)

    def sums(r, j):
        a, b = VSPANS[r][j]
        cp(v("acc", a, b), v("so", end(r, a) - 1, end(r, b - 1), 192))

    done = []

    def quad(i):
        ks, n, c0 = QUADS[i]
        quant(v("cc", c0, c0 + n), v("cs", c0, c0 + n), v("ct", 4 * c0, 4 * (c0 + n)))
        done.append(i)
        mm(SUMS, n, v("qb"), v("sb"), v("cc", c0, c0 + n), v("cs", c0, c0 + n),
           len(done) % len(QUADS) == 1, len(done) % len(QUADS) == 0)

    def signs(h, turn):
        n = 0
        for i, k in enumerate(turn):
            while n < min(len(turn), i + (2 if k > 12 else 3 if k > 7 else 4)):
                j = turn[n]
                act(v("sg", SG * j, SG * j + 16 * j), ps(SS[h], 16 * j), fn.Sign, bias=col("sx", 16 * j + 15), scale=-1.0)
                n += 1
            act(cmp_view(k, 0, 16 * k), v("sg", SG * k, SG * k + 16 * k), fn.Relu, acc=col("acc", k))

    def tastes(r):
        for j in range(4):
            mm(TASTE[j], C, uk(j)[0], uk(j)[1], v("qx%d" % r), v("sx%d" % r))

    def base(r):
        edges = [0] + [e for span in VSPANS[r] for e in span]
        for i, (a, b) in enumerate(zip(edges, edges[1:])):
            ts(v("base", 24 * r + a, 24 * r + b), v("num", 16 * a, 16 * b, 16), cq, op.subtract, 14.625 - 192 * (i % 2), op.add)

    def run(plan, r, more):
        steps = {"scores": lambda h: scores(r, h), "mask": mask, "keep": keep, "inner": inner, "sum": inner_sum,
                 "compare": compare, "count": lambda k: count(r, k), "sums": lambda j: sums(r, j), "quad": quad,
                 "pick": pick, "base": base, "signs": lambda j: signs(*SBLOCKS[r][j]), "tastes": lambda j: tastes(r),
                 "places": lambda j: tt(v("ra", 0, 24), v("base", 24 * r, 24 * r + 24), v("dr", 15, C, 16), op.subtract)}
        steps.update(more)
        for step in plan.split():
            name = step.rstrip("0123456789")
            steps[name](int(step[len(name):]))

    run(PLAN0, 0, {})
    for r in range(2):
        X, Y = xs[r], ys[r]
        act(v("cq"), ps(TASTE[1]), fn.Copy)
        act(v("cr"), ps(TASTE[2]), fn.Copy)
        if r == 0:
            later_constants()

        def test(out, bank, other, how, h):
            tt(v(out, H * h, H * h + H), v("ps%d" % bank, H * h, H * h + H), v(other, H * h, H * h + H), how)

        def lower(h):
            ts(v("y2", H * h, H * h + H), v("d2", H * h, H * h + H), col("col", 3), op.add, 0.0, op.is_gt)

        fills = [lambda h=h, a=a: test(*a, h) for a in (("d1", TASTE[0], "cq", op.subtract), ("mrt", TASTE[3], "cr", op.max),
                                                        ("d2", TASTE[0], "mrt", op.subtract)) for h in range(2)]
        fills[2:2] = [lambda: act(v("y1"), v("d1"), fn.Sign, bias=col("col", 2))]
        fills += [lambda: lower(0), lambda: lower(1)]

        def filler(n=1):
            for _ in range(min(n, len(fills))):
                fills.pop(0)()

        tt(v("ra", 24, 48), v("ra", 0, 24), v("acc"), op.subtract)
        if r == 0:
            pick(4)
        ts(v("ra", 48, 72), v("ra", 24, 48), 2.0 ** -13, op.mult)
        scan(v("ex"), ps(SUMS), v("sel16"), 0.0, op.add, op.mult)
        filler()
        tt(v("ra", 72, 96), v("ex", 15, C, 16), v("ra", 48, 72), op.add)
        filler()
        ts(v("rk"), v("ra", 72, 96), 8192.0, op.mult)
        filler(2)
        scatter(v("ord"), v("rk"), v("val"))
        filler()
        scan(v("osl"), v("ord", 0, 128), v("sel"), 0.0, op.add, op.mult)
        filler()
        ts(v("mo"), v("osl", 3, 128, 4), 8192.0, op.mult, -0.375, op.add)
        filler()
        mt = "mt%d" % r
        act(v(mt, 256, 512), ind(v(X), v("mo", 16, 32)), fn.Copy)
        cp(v(mt, 0, 256), ind(v(X), v("mo", 0, 16)))
        qm, sm, lq, ls = v("qm%d" % r), v("sm%d" % r), v("lq%d" % r), v("ls%d" % r)
        filler(2)
        quant(qm, sm, v(mt))
        wait("G", "V", total["V"])
        rid, pid = topo.addr(far[r])[:2]
        arr = "arr%d" % r
        g.remote_dma(lq[0].bitcast(dt.uint8), qm[0].bitcast(dt.uint8), T.sem[arr], T.sem.sent, pid, rid, topo.mask(core, far[r]))
        g.remote_dma(ls[0], sm[0], T.sem[arr], T.sem.sent, pid, rid, topo.mask(core, far[r]))

        def standing(j):
            tt(v("vk", A * j, A * j + A), v("cnt", A * j, A * j + A), v("ind", A * j, A * j + A), op.mult)

        if r == 0:
            pick_scales(4)
            fills += weights()
        tt(v("ind"), v("y1"), v("y2"), op.is_equal)
        filler()
        fill(v("alive", 0, A), 1.0)
        scan(v("cnt"), v("ind"), v("one", 0, C), col("col", 4), op.add, op.mult)
        filler()
        ts(col("mu", 0), col("cnt", C - 1), col("col", 5), op.add)
        filler()
        standing(0)
        tt(v("mrow", 16, 32), ind(v("num"), col("mu", 0)), v("wa"), op.mult)
        filler()
        standing(1)
        tt(v("mrow", 0, 16), v("mrow", 16, 32), v("wb"), op.add)

        def turn_standings():
            standing(2)
            wait("Y", "sent", sent[r])
            for h in range(2):
                for k in range(4):
                    dma("Y", "tr%d" % r, v("tin", 32 * k + 16 * h, 32 * k + 16 * h + 16),
                        v("vk", rows=slice(16 * h + k, 128, 32)))

        wait("P", arr, 2 * len(topo.engines(far[r], core)))
        mm(1, A, uk(4)[0], uk(4)[1], lq, ls)
        mm(0, A, uk(4)[0], uk(4)[1], lq, ls)

        def objects(b):
            qe, se = v("qe", 128 * b, 128 * b + 128), v("se", 128 * b, 128 * b + 128)
            if r == 0:
                quant(qe, se, v("et", 512 * b, 512 * b + 512))
            mm(2 + b, A, qe, se, lq, ls)

        def slots(b):
            ts(v("zo", 24 * b, 24 * b + 24), v("slot", 0, 24), 16.0, op.mult, 4.0 * b, op.add)

        spare = {
            1: [lambda b=b: objects(b) for b in range(3)],
            2: [lambda: objects(3)] + [lambda: quant(v("qv"), v("sv"), v("vt")), lambda: base(1)][2 * r:],
            4: [lambda: issue("V", lambda: g.vector.transpose(T.tout[:, :], T.tin[:, :]), [v("tout")], [v("tin")]),
                lambda: tt(v("s64"), v("tout", 0, 64), v("tout", 64, 128), op.add),
                lambda: tt(v("s32"), v("s64", 0, 32), v("s64", 32, 64), op.add)],
            5: [lambda: ts(v("fi"), v("s32"), 0.1, op.mult, -0.46, op.add),
                lambda: ts(v("f10"), v("fi"), -10.0, op.mult),
                lambda: tt(v("slot"), v("s32"), v("f10"), op.add)],
            6: [lambda b=b: slots(b) for b in range(3)],
            7: [lambda: slots(3)],
            8: [lambda: ts(v("ho", 0, 8), v("ee", 0, 8), 4.0, op.mult, cr, op.add)],
        }
        for t in range(TICKS):
            fills = list(spare.get(t, []))
            scan(v("rm"), ps(1, A) if t == 0 else v("msk", 0, A), v("low"), -BIG, op.max, op.max)
            act(v("step", 1, A + 1), v("rm"), fn.Sign, bias=col("rm", A - 1), scale=-1.0, acc=col("ee", t))
            if t == 0:
                act(v("msk", 0, A), ps(0, A), fn.Copy)
                turn_standings()
            if t < 4:
                act(v("xh", C * t, C * t + C), v(X, t, 4 * C, 4), fn.Identity, scale=0.5)
            elif t < 8:
                act(v("bh", t - 4, 512, 4), ps(t - 2, A), fn.Identity, scale=0.5)
                if r == 0:
                    act(v("ya", C * (t - 4), C * (t - 3)), v(X, t - 4, 4 * C, 4), fn.Identity, scale=32.0)
            if t + 1 == TICKS:
                break
            now = v("mrow", 0, 16) if t == 0 else v("ww", 16 * t, 16 * t + 16)
            if t > 0:
                old = v("mrow", 0, 16) if t == 1 else v("ww", 16 * t - 16, 16 * t)
                tt(v("wt", 16, 32), ind(v("alive"), col("o5", 4 * t - 2)), old, op.mult)
                tt(now, v("wt", 16, 32), v("mrow", 0, 16), op.add)
            ts(v("o5", 4 * t, 4 * t + 3), v("c5", 0, 3), col("ee", t), op.add, A + 1.0, op.min)
            tt(v("wt", 32, 48), ind(v("step"), col("o5", 4 * t)), now, op.mult)
            filler()
            minus_sum(col("sc", t), v("wt", 32, 48))
            filler()
            ts(col("o1", 2 * t), col("sc", t), col("ee", t), op.max, col("col", 7), op.min)
            filler()
            scatter(v("msk"), col("o1", 2 * t), v("low", 0, 16))
            if t + 2 < TICKS:
                scatter(v("alive"), col("o1", 2 * t), v("vk", C, C + 16))
            if t == 8:
                act(v("bm", 0, 128), ind(v("bh"), v("ho", 0, 8)), fn.Copy)

        ts(v("ho", 8, TICKS), v("ee", 8, TICKS), 4.0, op.mult, cr, op.add)
        if r == 1:
            cp(v("ho2"), v("ee", 0, TICKS))
        cp(v("bm", 128, 160), ind(v("bh"), v("ho", 8, TICKS)))
        zt = "zt%d" % r
        Xn, Yn, qn, sn = xs[r + 1], ys[r + 1], "qx%d" % (r + 1), "sx%d" % (r + 1)

        def planar(name, j):
            (a, e), b = CUTS[j // 4], j % 4
            return v(name, C * b + a, C * b + e)

        def tiled(name, j):
            (a, e), b = CUTS[j // 4], j % 4
            return v(name, 4 * a + b, 4 * e, 4)

        def chosen(j):
            (a, e), b = CUTS[j // 4], j % 4
            return ind(v("bm"), v("zo", 24 * b + a // 16, 24 * b + e // 16))

        for j in FETCH:
            act(planar("got", j), chosen(j), fn.Copy)

        def take(j):
            tt(tiled(zt, j), planar("got", j) if j in FETCH else chosen(j), planar("xh", j), op.add)

        def layer(h):
            a, e = CUTS[h]
            qz, sz = v("qz%d" % r, a, e), v("sz%d" % r, a, e)
            quant(qz, sz, v(zt, 4 * a, 4 * e))
            for b in range(4):
                mm(LAYER[h][b], e - a, v("qw", 128 * b, 128 * b + 128), v("sw", 128 * b, 128 * b + 128), qz, sz)

        def renew(j):
            tt(planar(Yn, j), ps(LAYER[j // 4][j % 4], A), planar(Y, j), op.add)
            if j not in OWN[r]:
                act(tiled(Xn, j), planar(Yn, j), fn.Identity, scale=1.0 / 32)

        def shrink(j):
            ts(tiled(Xn, j), planar(Yn, j), 1.0 / 32, op.mult)

        def lists(j):
            if j == 0:
                act(v("erow"), ind(v("num"), v("ho2")), fn.Copy)
            else:
                act(v("lrow"), ind(v("erow"), v("zo", 0, 24)), fn.Copy)

        def codes(h):
            a, e = CUTS[h]
            quant(v(qn, a, e), v(sn, a, e), v(Xn, 4 * a, 4 * e))
            mm(LAST[h], e - a, v("qv"), v("sv"), v(qn, a, e), v(sn, a, e))
            dma("Y", "out", (T.oc[:, 4 * a:4 * e], []), bytes_of(v(qn, a, e)))

        def store(h):
            a, e = CUTS[h]
            act(v("yo", a, e), ps(LAST[h], e - a), fn.Copy)
            dma("S", "out", (T.y[:, a:e], []), v("yo", a, e))

        run(PLAN1 if r + 1 < len(STEPS) else PLAN2, r + 1,
            {"take": take, "layer": layer, "renew": renew, "shrink": shrink, "lists": lists, "codes": codes, "store": store})
    for k in range(4):
        dma("Y", "out", (T.osc[4 * k:4 * k + 4, :], []), v("sx2", rows=slice(32 * k, 32 * k + 4)))
    dma("Y", "out", (T.ol[:, :], []), v("lrow", rows=slice(0, 128, 16)))
    g.wait_ge(T.sem.sent, sent[-1])
    for sem in sorted(total):
        wait("G", sem, total[sem])
